import numpy as np
import ml_dtypes


def mxq(x, axis, fmt="e4m3"):
    dtype, down = {"e4m3": (ml_dtypes.float8_e4m3fn, 7), "e5m2": (ml_dtypes.float8_e5m2, 14)}[fmt]
    v = np.moveaxis(np.asarray(x, np.float32).astype(ml_dtypes.bfloat16).astype(np.float64), axis, -1)
    blocks = v.reshape(v.shape[:-1] + (-1, 32))
    amax = np.abs(blocks).max(-1, keepdims=True)
    byte = np.maximum(np.where(amax > 0, np.frexp(amax)[1] - 1 + 127, 0) - down, 1)
    scale = np.exp2(byte - 127.0)
    codes = (blocks / scale).astype(np.float32).astype(dtype).astype(np.float64)
    return np.moveaxis((codes * scale).reshape(v.shape), -1, axis)


WIDE = False


def mx_kscale(k):
    if not WIDE:
        return np.ones(k)
    levels = np.array([10, -10, 5, -5, 0])
    if k % 512:
        return np.exp2(np.random.permutation(np.resize(levels, k // 32))).repeat(32)
    a = np.empty((k // 512, 16))
    for p in range(k // 512):
        a[p, :8] = np.random.permutation(np.resize(levels, 8))
        for g in range(8):
            far = levels[np.abs(levels - a[p, g]) >= 10]
            a[p, g + 8] = far[np.random.randint(len(far))]
    return np.exp2(a.ravel()).repeat(32)


def f64(x):
    return np.asarray(x).astype(np.float64)


def striped(idx):
    return np.tile(idx.reshape(-1, 16).T, (8, 1)).astype(np.uint16)


def unstriped(offs):
    return offs[:16].T.reshape(-1).astype(np.int64)


def pack_weight(w):
    k, n = w.shape
    w = f64(np.asarray(w, np.float32).astype(ml_dtypes.bfloat16)).reshape(k // 32, 32, n)
    amax = np.abs(w).max(1)
    byte = np.clip(np.where(amax > 0, np.frexp(amax)[1] - 1 + 127 - 7, 1), 1, 254)
    scaled = (w * np.exp2(127.0 - byte)[:, None, :]).reshape(k, n).astype(np.float32)
    words = np.ascontiguousarray(scaled.reshape(k // 512, 128, 4, n).transpose(0, 1, 3, 2)).astype(ml_dtypes.float8_e4m3fn).view(np.uint8)
    return words, np.ascontiguousarray(byte.astype(np.uint8).reshape(k // 512, 16, n))


def unpack_weight(words, scales):
    g, p, n, _ = words.shape
    vals = np.ascontiguousarray(words).view(ml_dtypes.float8_e4m3fn).astype(np.float64) * np.repeat(np.exp2(scales.astype(np.float64) - 127.0), 8, axis=1)[..., None]
    return vals.transpose(0, 1, 3, 2).reshape(g * 512, n)


def relu(v):
    return np.maximum(v, 0.0)


K, T, S, V, H, N = 512, 1024, 512, 256, 512, 128


def setup_inputs():
    n = np.random.standard_normal
    s = mx_kscale(K)[:, None]
    u = mx_kscale(H)
    packed_w3 = pack_weight(n((H, N)) / np.sqrt(H) / u[:, None])
    return {
        "xT": (n((K, T)) * s).astype(np.float32),
        "w1": (n((K, H)) / np.sqrt(2 * K) / s * u).astype(np.float32),
        "w2": (n((K, H)) / np.sqrt(2 * K) / s * u).astype(np.float32),
        "w3_words": packed_w3[0],
        "w3_scales": packed_w3[1],
        "offs": striped(np.random.permutation(T)[:S]),
        "cen": striped(np.random.permutation(S)[:V]),
        "pos1": striped(np.random.permutation(S)[:V]),
        "pos2": striped(np.random.permutation(S)[:V]),
        "pos3": striped(np.random.permutation(S)[:V]),
        "pos4": striped(np.random.permutation(S)[:V]),
    }


def reference(xT, w1, w2, w3_words, w3_scales, offs, cen, pos1, pos2, pos3, pos4):
    xq = mxq(f64(xT)[:, unstriped(offs)], 0, "e4m3")
    y = mxq(f64(w1), 0, "e4m3").T @ xq
    yc = y[:, unstriped(cen)]
    e = mxq(f64(w2), 0, "e4m3").T @ xq
    z = np.maximum(np.maximum(np.maximum(relu(yc + e[:, unstriped(pos1)]), relu(yc + e[:, unstriped(pos2)])), relu(yc + e[:, unstriped(pos3)])), relu(yc + e[:, unstriped(pos4)]))
    return unpack_weight(w3_words, w3_scales).T @ mxq(z, 0, "e4m3")

@@ -1,0 +1,227 @@
+from contextlib import ExitStack
+
+import concourse.mybir as mybir
+
+K, T, S, V, H, N = 512, 1024, 512, 256, 512, 128
+FLOPS = 2 * K * H * S * 2 + 2 * H * N * V
+
+F32 = mybir.dt.float32
+BF16 = mybir.dt.bfloat16
+U32 = mybir.dt.uint32
+I32 = mybir.dt.int32
+U16 = mybir.dt.uint16
+U8 = mybir.dt.uint8
+FP8X4 = mybir.dt.float8_e4m3fn_x4
+ADD = mybir.AluOpType.add
+MAX = mybir.AluOpType.max
+RELU = mybir.ActivationFunctionType.Relu
+
+P = 128
+PACK = 4
+HALF_S = S // 2
+HALF_V = V // 2
+
+
+def tile_picked_edgecv_relu_e_kernel(
+    tc, xT, w1, w2, w3_words, w3_scales, offs, cen, pos1, pos2, pos3, pos4, out
+):
+    nc = tc.nc
+    with ExitStack() as ctx:
+        keep = ctx.enter_context(tc.tile_pool(name="keep", bufs=1))
+        psum = ctx.enter_context(tc.psum_pool(name="psum", bufs=1))
+
+        def load_list(source, name):
+            tile = keep.tile(list(source.shape), U16, name=name)
+            nc.sync.dma_start(tile[:], source)
+            return tile
+
+        x_rows = xT.rearrange("(p u e) c -> p u e c", u=2, e=2)
+
+        def load_x(u, c0, c1):
+            raw = keep.tile([P, 2, c1 - c0], F32, name="x_raw_%d_%d" % (u, c0))
+            nc.sync.dma_start(raw[:], x_rows[:, u, :, c0:c1])
+            return raw
+
+        def load_w(w, half, name):
+            raw = keep.tile([P, PACK, H // 2], F32, name="%s_raw_%d" % (name, half))
+            nc.sync.dma_start(raw[:], w.rearrange("(p j) c -> p j c", j=PACK)[:, :, half * (H // 2) : (half + 1) * (H // 2)])
+            return raw
+
+        x_chunks = [(0, 0, 512), (0, 512, 1024), (1, 0, 512), (1, 512, 768), (1, 768, 1024)]
+        x_raw = [load_x(*x_chunks[0])]
+        offs_sb = load_list(offs, "offs_sb")
+        x_raw.extend(load_x(*chunk) for chunk in x_chunks[1:])
+        w2_raw = [load_w(w2, half, "w2") for half in range(2)]
+        pos_sb = [load_list(pos, "pos_sb_%d" % d) for d, pos in enumerate((pos1, pos2, pos3, pos4))]
+        w1_raw = [load_w(w1, half, "w1") for half in range(2)]
+        cen_sb = load_list(cen, "cen_sb")
+
+        w3_codes = keep.tile([P, N], U32, align_bytes=64)
+        nc.sync.dma_start(w3_codes[:].bitcast(I32), w3_words[0].rearrange("p n t -> p (n t)").bitcast(I32))
+        w3_plane = keep.tile([P, N], U8, align_bytes=64)
+        nc.gpsimd.memset(w3_plane[:], 0)
+        for q in range(4):
+            nc.sync.dma_start(w3_plane[32 * q : 32 * q + 4, :].bitcast(I32), w3_scales[0, 4 * q : 4 * q + 4, :].bitcast(I32))
+
+        x_pairs = [keep.tile([P, T, 2], BF16, name="x_pairs_%d" % u) for u in range(2)]
+        x_picked = [keep.tile([P, HALF_S, 2], U32, name="x_picked_%d" % h, align_bytes=64) for h in range(2)]
+        x_codes = keep.tile([P, S], U32, align_bytes=64)
+        x_plane = keep.tile([P, S], U8, align_bytes=64)
+
+        def pair_x(index, copy):
+            u, c0, c1 = x_chunks[index]
+            copy(
+                x_pairs[u][:, c0:c1, :].rearrange("p (c i) e -> p c e i", i=4),
+                x_raw[index][:].rearrange("p e (c i) -> p c e i", i=4),
+            )
+
+        def pick_x(u, h):
+            window = x_pairs[u][:].rearrange("p c e -> p (c e)").bitcast(U32)
+            nc.vector.tensor_copy(x_picked[h][:, :, u], window.indirect(offs_sb[:, 16 * h : 16 * (h + 1)]))
+
+        def quantize_x(h):
+            cols = slice(h * HALF_S, (h + 1) * HALF_S)
+            nc.vector.quantize_mx(
+                out=x_codes[:, cols].bitcast(FP8X4),
+                scales=x_plane[:, cols],
+                in_=x_picked[h][:].rearrange("p c u -> p (c u)").bitcast(BF16),
+            )
+
+        def deal_w(raw, dealt, half, t0, t1, copy):
+            m = slice(half * 64, (half + 1) * 64)
+            copy(
+                dealt[:, t0:t1, m, :].rearrange("p t m j -> p m j t"),
+                raw[half][:].rearrange("p j (m t) -> p m j t", t=PACK)[:, :, :, t0:t1],
+            )
+
+        def quantize_w(dealt, codes, plane, t0, t1):
+            cols = slice(t0 * P, t1 * P)
+            nc.vector.quantize_mx(
+                out=codes[:, cols].bitcast(FP8X4),
+                scales=plane[:, cols],
+                in_=dealt[:, t0:t1, :, :].rearrange("p t m j -> p (t m j)"),
+            )
+
+        def product(acc, codes, plane, t, cols):
+            nc.tensor.matmul_mx(
+                out=acc,
+                lhsT=codes[:, t * P : (t + 1) * P].bitcast(FP8X4),
+                lhsT_scale=plane[:, t * P : (t + 1) * P],
+                rhs=x_codes[:, cols].bitcast(FP8X4),
+                rhs_scale=x_plane[:, cols],
+                start=True,
+                stop=True,
+            )
+
+        w2_first = keep.tile([P, 1, P, PACK], BF16, align_bytes=64)
+        w2_dealt = keep.tile([P, PACK, P, PACK], BF16, align_bytes=64)
+        w1_dealt = keep.tile([P, PACK, P, PACK], BF16, align_bytes=64)
+        w2_codes = keep.tile([P, H], U32, align_bytes=64)
+        w2_plane = keep.tile([P, H], U8, align_bytes=64)
+        w1_codes = keep.tile([P, H], U32, align_bytes=64)
+        w1_plane = keep.tile([P, H], U8, align_bytes=64)
+
+        pair_x(0, nc.vector.tensor_copy)
+        pair_x(1, nc.vector.tensor_copy)
+        pick_x(0, 0)
+        pick_x(0, 1)
+        pair_x(2, nc.scalar.copy)
+        pair_x(3, nc.scalar.copy)
+        pair_x(4, nc.vector.tensor_copy)
+        pick_x(1, 0)
+        pick_x(1, 1)
+        quantize_x(0)
+        quantize_x(1)
+
+        deal_w(w2_raw, w2_first, 0, 0, 1, nc.scalar.copy)
+        deal_w(w2_raw, w2_dealt, 0, 1, PACK, nc.scalar.copy)
+        deal_w(w2_raw, w2_first, 1, 0, 1, nc.scalar.copy)
+        quantize_w(w2_first, w2_codes, w2_plane, 0, 1)
+
+        e_rows = [keep.tile([P, S], F32, name="e_rows_%d" % t) for t in range(PACK)]
+        y_rows = [keep.tile([P, S], F32, name="y_rows_%d" % t) for t in range(PACK)]
+
+        for h, copy in enumerate((nc.scalar.copy, nc.vector.tensor_copy)):
+            cols = slice(h * HALF_S, (h + 1) * HALF_S)
+            acc_half = psum.tile([P, HALF_S], F32, name="acc_half", bufs=2)
+            product(acc_half[:], w2_codes, w2_plane, 0, cols)
+            copy(e_rows[0][:, cols], acc_half[:])
+
+        deal_w(w2_raw, w2_dealt, 1, 1, PACK, nc.vector.tensor_copy)
+        quantize_w(w2_dealt, w2_codes, w2_plane, 1, 2)
+        quantize_w(w2_dealt, w2_codes, w2_plane, 2, 4)
+        for t in range(1, PACK):
+            acc = psum.tile([P, S], F32, name="acc", bufs=4)
+            product(acc[:], w2_codes, w2_plane, t, slice(0, S))
+            nc.scalar.copy(e_rows[t][:], acc[:])
+
+        for half in range(2):
+            deal_w(w1_raw, w1_dealt, half, 0, PACK, nc.scalar.copy)
+
+        fetched = [keep.tile([P, 4, V], F32, name="fetched_%d" % t) for t in range(PACK)]
+        pair_max = [keep.tile([P, 2, V], F32, name="pair_max_%d" % t) for t in range(PACK)]
+        largest = [keep.tile([P, V], F32, name="largest_%d" % t) for t in range(PACK)]
+        summed = keep.tile([P, PACK, V], F32)
+
+        def fetch(t, d):
+            nc.vector.tensor_copy(fetched[t][:, d, :], e_rows[t][:].indirect(pos_sb[d][:]))
+
+        def max_pairs(t):
+            nc.vector.tensor_tensor(pair_max[t][:], fetched[t][:, 0:2, :], fetched[t][:, 2:4, :], MAX)
+
+        def max_last(t):
+            nc.vector.tensor_tensor(largest[t][:], pair_max[t][:, 0, :], pair_max[t][:, 1, :], MAX)
+
+        def add_centre(t, v0, v1):
+            nc.vector.tensor_tensor(summed[:, t, v0:v1], y_rows[t][:].indirect(cen_sb[:, v0 // 16 : v1 // 16]), largest[t][:, v0:v1], ADD)
+
+        for d in range(4):
+            fetch(0, d)
+        quantize_w(w1_dealt, w1_codes, w1_plane, 0, PACK)
+        for t in range(PACK):
+            acc = psum.tile([P, S], F32, name="acc", bufs=4)
+            product(acc[:], w1_codes, w1_plane, t, slice(0, S))
+            nc.scalar.copy(y_rows[t][:], acc[:])
+        for t in range(1, PACK):
+            fetch(t, 0)
+            max_pairs(t - 1)
+            fetch(t, 1)
+            max_last(t - 1)
+            fetch(t, 2)
+            fetch(t, 3)
+        add_centre(0, 0, V)
+        max_pairs(PACK - 1)
+        add_centre(1, 0, V)
+        max_last(PACK - 1)
+        add_centre(2, 0, V)
+
+        for h in range(2):
+            v0, v1 = h * HALF_V, (h + 1) * HALF_V
+            add_centre(PACK - 1, v0, v1)
+        z_woven = [keep.tile([P, HALF_V, PACK], BF16, name="z_woven_%d" % h, align_bytes=64) for h in range(2)]
+        for h in range(2):
+            v0, v1 = h * HALF_V, (h + 1) * HALF_V
+            woven = z_woven[h][:].rearrange("p (c i) t -> p c t i", i=4)
+            source = summed[:, :, v0:v1].rearrange("p t (c i) -> p c t i", i=4)
+            if h == 0:
+                nc.scalar.activation(woven, source, RELU)
+            else:
+                nc.vector.tensor_scalar_max(woven, source, 0.0)
+        for h in range(2):
+            v0, v1 = h * HALF_V, (h + 1) * HALF_V
+            z_codes = keep.tile([P, HALF_V], U32, name="z_codes_%d" % h, align_bytes=64)
+            z_plane = keep.tile([P, HALF_V], U8, name="z_plane_%d" % h, align_bytes=64)
+            nc.vector.quantize_mx(out=z_codes[:].bitcast(FP8X4), scales=z_plane[:], in_=z_woven[h][:].rearrange("p v t -> p (v t)"))
+            acc_out = psum.tile([P, HALF_V], F32, name="acc_out", bufs=2)
+            nc.tensor.matmul_mx(
+                out=acc_out[:],
+                lhsT=w3_codes[:].bitcast(FP8X4),
+                lhsT_scale=w3_plane[:],
+                rhs=z_codes[:].bitcast(FP8X4),
+                rhs_scale=z_plane[:],
+                start=True,
+                stop=True,
+            )
+            result = keep.tile([P, HALF_V], F32, name="result_%d" % h)
+            nc.scalar.copy(result[:], acc_out[:])
+            nc.sync.dma_start(out[:, v0:v1], result[:])

@@ -42,18 +42,18 @@ def tile_picked_edgecv_relu_e_kernel(
             nc.sync.dma_start(raw[:], x_rows[:, u, :, c0:c1])
             return raw
 
-        def load_w(w, half, name):
-            raw = keep.tile([P, PACK, H // 2], F32, name="%s_raw_%d" % (name, half))
-            nc.sync.dma_start(raw[:], w.rearrange("(p j) c -> p j c", j=PACK)[:, :, half * (H // 2) : (half + 1) * (H // 2)])
+        def load_w(w, j0, j1, name):
+            raw = keep.tile([P, j1 - j0, H], F32, name="%s_raw_%d" % (name, j0))
+            nc.sync.dma_start(raw[:], w.rearrange("(p j) c -> p j c", j=PACK)[:, j0:j1, :])
             return raw
 
-        x_chunks = [(0, 0, 512), (0, 512, 1024), (1, 0, 512), (1, 512, 768), (1, 768, 1024)]
+        x_chunks = [(0, 0, 1024), (1, 0, 512), (1, 512, 1024)]
         x_raw = [load_x(*x_chunks[0])]
         offs_sb = load_list(offs, "offs_sb")
         x_raw.extend(load_x(*chunk) for chunk in x_chunks[1:])
-        w2_raw = [load_w(w2, half, "w2") for half in range(2)]
+        w2_raw = [load_w(w2, 2 * u, 2 * u + 2, "w2") for u in range(2)]
         pos_sb = [load_list(pos, "pos_sb_%d" % d) for d, pos in enumerate((pos1, pos2, pos3, pos4))]
-        w1_raw = [load_w(w1, half, "w1") for half in range(2)]
+        w1_raw = load_w(w1, 0, PACK, "w1")
         cen_sb = load_list(cen, "cen_sb")
 
         w3_codes = keep.tile([P, N], U32, align_bytes=64)
@@ -68,11 +68,11 @@ def tile_picked_edgecv_relu_e_kernel(
         x_codes = keep.tile([P, S], U32, align_bytes=64)
         x_plane = keep.tile([P, S], U8, align_bytes=64)
 
-        def pair_x(index, copy):
-            u, c0, c1 = x_chunks[index]
+        def pair_x(index, c0, c1, copy):
+            u, base = x_chunks[index][0:2]
             copy(
-                x_pairs[u][:, c0:c1, :].rearrange("p (c i) e -> p c e i", i=4),
-                x_raw[index][:].rearrange("p e (c i) -> p c e i", i=4),
+                x_pairs[u][:, base + c0 : base + c1, :].rearrange("p (c i) e -> p c e i", i=4),
+                x_raw[index][:, :, c0:c1].rearrange("p e (c i) -> p c e i", i=4),
             )
 
         def pick_x(u, h):
@@ -87,11 +87,10 @@ def tile_picked_edgecv_relu_e_kernel(
                 in_=x_picked[h][:].rearrange("p c u -> p (c u)").bitcast(BF16),
             )
 
-        def deal_w(raw, dealt, half, t0, t1, copy):
-            m = slice(half * 64, (half + 1) * 64)
+        def deal_w(raw, j0, dealt, t0, t1, m0, m1, copy):
             copy(
-                dealt[:, t0:t1, m, :].rearrange("p t m j -> p m j t"),
-                raw[half][:].rearrange("p j (m t) -> p m j t", t=PACK)[:, :, :, t0:t1],
+                dealt[:, :, m0:m1, j0 : j0 + raw.shape[1]].rearrange("p t m j -> p m j t"),
+                raw[:].rearrange("p j (m t) -> p m j t", t=PACK)[:, m0:m1, :, t0:t1],
             )
 
         def quantize_w(dealt, codes, plane, t0, t1):
@@ -99,7 +98,7 @@ def tile_picked_edgecv_relu_e_kernel(
             nc.vector.quantize_mx(
                 out=codes[:, cols].bitcast(FP8X4),
                 scales=plane[:, cols],
-                in_=dealt[:, t0:t1, :, :].rearrange("p t m j -> p (t m j)"),
+                in_=dealt.rearrange("p t m j -> p (t m j)"),
             )
 
         def product(acc, codes, plane, t, cols):
@@ -113,30 +112,34 @@ def tile_picked_edgecv_relu_e_kernel(
                 stop=True,
             )
 
-        w2_first = keep.tile([P, 1, P, PACK], BF16, align_bytes=64)
-        w2_dealt = keep.tile([P, PACK, P, PACK], BF16, align_bytes=64)
-        w1_dealt = keep.tile([P, PACK, P, PACK], BF16, align_bytes=64)
         w2_codes = keep.tile([P, H], U32, align_bytes=64)
         w2_plane = keep.tile([P, H], U8, align_bytes=64)
         w1_codes = keep.tile([P, H], U32, align_bytes=64)
         w1_plane = keep.tile([P, H], U8, align_bytes=64)
 
-        pair_x(0, nc.vector.tensor_copy)
-        pair_x(1, nc.vector.tensor_copy)
+        pair_x(0, 0, 640, nc.vector.tensor_copy)
+        pair_x(0, 640, 1024, nc.scalar.copy)
         pick_x(0, 0)
         pick_x(0, 1)
-        pair_x(2, nc.scalar.copy)
-        pair_x(3, nc.scalar.copy)
-        pair_x(4, nc.vector.tensor_copy)
+        pair_x(1, 0, 512, nc.scalar.copy)
+        pair_x(2, 0, 352, nc.vector.tensor_copy)
+        pair_x(2, 352, 512, nc.scalar.copy)
         pick_x(1, 0)
         pick_x(1, 1)
         quantize_x(0)
         quantize_x(1)
 
-        deal_w(w2_raw, w2_first, 0, 0, 1, nc.scalar.copy)
-        deal_w(w2_raw, w2_dealt, 0, 1, PACK, nc.scalar.copy)
-        deal_w(w2_raw, w2_first, 1, 0, 1, nc.scalar.copy)
-        quantize_w(w2_first, w2_codes, w2_plane, 0, 1)
+        w2_first = keep.tile([P, 1, P, PACK], BF16, tag="w2_dealt", align_bytes=64)
+        w2_last = keep.tile([P, 2, P, PACK], BF16, align_bytes=64)
+        for u in range(2):
+            deal_w(w2_raw[u], 2 * u, w2_first, 0, 1, 0, P, nc.scalar.copy)
+        deal_w(w2_raw[0], 0, w2_last, 2, 4, 0, 64, nc.scalar.copy)
+        deal_w(w2_raw[0], 0, w2_last, 2, 4, 64, P, nc.scalar.copy)
+        deal_w(w2_raw[1], 2, w2_last, 2, 4, 0, P, nc.scalar.copy)
+        quantize_w(w2_first[:], w2_codes, w2_plane, 0, 1)
+        w2_middle = keep.tile([P, 1, P, PACK], BF16, tag="w2_dealt", align_bytes=64)
+        for u in range(2):
+            deal_w(w2_raw[u], 2 * u, w2_middle, 1, 2, 0, P, nc.vector.tensor_copy)
 
         e_rows = [keep.tile([P, S], F32, name="e_rows_%d" % t) for t in range(PACK)]
         y_rows = [keep.tile([P, S], F32, name="y_rows_%d" % t) for t in range(PACK)]
@@ -147,68 +150,89 @@ def tile_picked_edgecv_relu_e_kernel(
             product(acc_half[:], w2_codes, w2_plane, 0, cols)
             copy(e_rows[0][:, cols], acc_half[:])
 
-        deal_w(w2_raw, w2_dealt, 1, 1, PACK, nc.vector.tensor_copy)
-        quantize_w(w2_dealt, w2_codes, w2_plane, 1, 2)
-        quantize_w(w2_dealt, w2_codes, w2_plane, 2, 4)
+
+        quantize_w(w2_middle[:], w2_codes, w2_plane, 1, 2)
+        quantize_w(w2_last[:], w2_codes, w2_plane, 2, 4)
         for t in range(1, PACK):
             acc = psum.tile([P, S], F32, name="acc", bufs=4)
             product(acc[:], w2_codes, w2_plane, t, slice(0, S))
             nc.scalar.copy(e_rows[t][:], acc[:])
 
-        for half in range(2):
-            deal_w(w1_raw, w1_dealt, half, 0, PACK, nc.scalar.copy)
+        w1_high = keep.tile([P, 2, P, PACK], BF16, tag="w1_high", align_bytes=64)
+        w1_low = keep.tile([P, 2, P, PACK], BF16, align_bytes=64)
+        for dealt, t0 in ((w1_high, 2), (w1_low, 0)):
+            for m0 in (0, 64):
+                deal_w(w1_raw, 0, dealt, t0, t0 + 2, m0, m0 + 64, nc.scalar.copy)
 
-        fetched = [keep.tile([P, 4, V], F32, name="fetched_%d" % t) for t in range(PACK)]
-        pair_max = [keep.tile([P, 2, V], F32, name="pair_max_%d" % t) for t in range(PACK)]
-        largest = [keep.tile([P, V], F32, name="largest_%d" % t) for t in range(PACK)]
-        summed = keep.tile([P, PACK, V], F32)
+        fetched = keep.tile([P, 4, V], F32)
+        early = keep.tile([P, 2, V], F32)
+        pair_max = [keep.tile([P, 2, V], F32, name="pair_max_%d" % t) for t in range(2)]
+        largest = keep.tile([P, 2, V], F32)
+        summed = keep.tile([P, 2, V], F32)
+        centre = {t: keep.tile([P, V], F32, name="centre_%d" % t) for t in (2, 3)}
+        edge = [keep.tile([P, 2, V], F32, name="edge_%d" % d) for d in range(3)]
+        high = [keep.tile([P, V, 2], BF16, name="high_%d" % d) for d in range(3)]
+        high_max = [keep.tile([P, V, 2], BF16, name="high_max_%d" % d) for d in range(2)]
+        z_woven = [keep.tile([P, HALF_V, PACK], BF16, name="z_woven_%d" % h, align_bytes=64) for h in range(2)]
 
-        def fetch(t, d):
-            nc.vector.tensor_copy(fetched[t][:, d, :], e_rows[t][:].indirect(pos_sb[d][:]))
+        def whole_product(rows, codes, plane, t):
+            acc = psum.tile([P, S], F32, name="acc", bufs=4)
+            product(acc[:], codes, plane, t, slice(0, S))
+            nc.scalar.copy(rows[t][:], acc[:])
 
-        def max_pairs(t):
-            nc.vector.tensor_tensor(pair_max[t][:], fetched[t][:, 0:2, :], fetched[t][:, 2:4, :], MAX)
+        def fetch(target, t, d):
+            nc.vector.tensor_copy(target, e_rows[t][:].indirect(pos_sb[d][:]))
 
-        def max_last(t):
-            nc.vector.tensor_tensor(largest[t][:], pair_max[t][:, 0, :], pair_max[t][:, 1, :], MAX)
+        def fetch_edge(target, t, d, v0, v1):
+            nc.vector.tensor_tensor(target, e_rows[t][:].indirect(pos_sb[d][:, v0 // 16 : v1 // 16]), centre[t][:, v0:v1], ADD)
 
-        def add_centre(t, v0, v1):
-            nc.vector.tensor_tensor(summed[:, t, v0:v1], y_rows[t][:].indirect(cen_sb[:, v0 // 16 : v1 // 16]), largest[t][:, v0:v1], ADD)
+        def weave(target, source):
+            nc.scalar.activation(
+                target.rearrange("p (c i) t -> p c t i", i=4), source.rearrange("p t (c i) -> p c t i", i=4), RELU
+            )
+
+        def larger(target, a, b):
+            nc.vector.tensor_tensor(target, a, b, MAX)
 
         for d in range(4):
-            fetch(0, d)
-        quantize_w(w1_dealt, w1_codes, w1_plane, 0, PACK)
-        for t in range(PACK):
-            acc = psum.tile([P, S], F32, name="acc", bufs=4)
-            product(acc[:], w1_codes, w1_plane, t, slice(0, S))
-            nc.scalar.copy(y_rows[t][:], acc[:])
-        for t in range(1, PACK):
-            fetch(t, 0)
-            max_pairs(t - 1)
-            fetch(t, 1)
-            max_last(t - 1)
-            fetch(t, 2)
-            fetch(t, 3)
-        add_centre(0, 0, V)
-        max_pairs(PACK - 1)
-        add_centre(1, 0, V)
-        max_last(PACK - 1)
-        add_centre(2, 0, V)
+            fetch(fetched[:, d, :], 0, d)
+        fetch(early[:, 0, :], 1, 0)
+        larger(pair_max[0][:], fetched[:, 0:2, :], fetched[:, 2:4, :])
+        fetch(early[:, 1, :], 1, 1)
+        quantize_w(w1_high[:], w1_codes, w1_plane, 2, 4)
+        larger(largest[:, 0, :], pair_max[0][:, 0, :], pair_max[0][:, 1, :])
+        for t in (2, 3):
+            whole_product(y_rows, w1_codes, w1_plane, t)
+        late = keep.tile([P, 2, V], F32, tag="w1_high", align_bytes=64)
+        fetch(late[:, 0, :], 1, 2)
+        fetch(late[:, 1, :], 1, 3)
+        quantize_w(w1_low[:], w1_codes, w1_plane, 0, 2)
+        larger(pair_max[1][:], early[:], late[:])
+        for t in range(2):
+            whole_product(y_rows, w1_codes, w1_plane, t)
+        nc.vector.tensor_copy(centre[2][:], y_rows[2][:].indirect(cen_sb[:]))
+        larger(largest[:, 1, :], pair_max[1][:, 0, :], pair_max[1][:, 1, :])
+        nc.vector.tensor_copy(centre[3][:], y_rows[3][:].indirect(cen_sb[:]))
+        for d in range(3):
+            for t in (2, 3):
+                fetch_edge(edge[d][:, t - 2, :], t, d, 0, V)
+            weave(high[d][:], edge[d][:])
+        for t in range(2):
+            nc.vector.tensor_tensor(summed[:, t, :], y_rows[t][:].indirect(cen_sb[:]), largest[:, t, :], ADD)
+        for h in range(2):
+            weave(z_woven[h][:, :, 0:2], summed[:, :, h * HALF_V : (h + 1) * HALF_V])
 
-        for h in range(2):
-            v0, v1 = h * HALF_V, (h + 1) * HALF_V
-            add_centre(PACK - 1, v0, v1)
-        z_woven = [keep.tile([P, HALF_V, PACK], BF16, name="z_woven_%d" % h, align_bytes=64) for h in range(2)]
-        for h in range(2):
-            v0, v1 = h * HALF_V, (h + 1) * HALF_V
-            woven = z_woven[h][:].rearrange("p (c i) t -> p c t i", i=4)
-            source = summed[:, :, v0:v1].rearrange("p t (c i) -> p c t i", i=4)
-            if h == 0:
-                nc.scalar.activation(woven, source, RELU)
-            else:
-                nc.vector.tensor_scalar_max(woven, source, 0.0)
-        for h in range(2):
-            v0, v1 = h * HALF_V, (h + 1) * HALF_V
+        def last_edge(t, h):
+            fetch_edge(edge[1 + h][:, t - 2, 0:HALF_V], t, 3, h * HALF_V, (h + 1) * HALF_V)
+
+        def finish_z(h):
+            larger(
+                z_woven[h][:, :, 2:4].rearrange("p (c i) t -> p c t i", i=4),
+                edge[1 + h][:, :, 0:HALF_V].rearrange("p t (c i) -> p c t i", i=4),
+                high_max[1][:, h * HALF_V : (h + 1) * HALF_V, :].rearrange("p (c i) t -> p c t i", i=4),
+            )
+
+        def project(h):
             z_codes = keep.tile([P, HALF_V], U32, name="z_codes_%d" % h, align_bytes=64)
             z_plane = keep.tile([P, HALF_V], U8, name="z_plane_%d" % h, align_bytes=64)
             nc.vector.quantize_mx(out=z_codes[:].bitcast(FP8X4), scales=z_plane[:], in_=z_woven[h][:].rearrange("p v t -> p (v t)"))
@@ -224,4 +248,15 @@ def tile_picked_edgecv_relu_e_kernel(
             )
             result = keep.tile([P, HALF_V], F32, name="result_%d" % h)
             nc.scalar.copy(result[:], acc_out[:])
-            nc.sync.dma_start(out[:, v0:v1], result[:])
+            nc.sync.dma_start(out[:, h * HALF_V : (h + 1) * HALF_V], result[:])
+
+        larger(high_max[0][:], high[0][:], high[1][:])
+        last_edge(2, 0)
+        last_edge(3, 0)
+        larger(high_max[1][:], high_max[0][:], high[2][:])
+        last_edge(2, 1)
+        finish_z(0)
+        last_edge(3, 1)
+        project(0)
+        finish_z(1)
+        project(1)

@@ -35,31 +35,53 @@ def tile_picked_edgecv_relu_e_kernel(
             nc.sync.dma_start(tile[:], source)
             return tile
 
-        x_rows = xT.rearrange("(p u e) c -> p u e c", u=2, e=2)
-
-        def load_x(u, c0, c1):
-            raw = keep.tile([P, 2, c1 - c0], F32, name="x_raw_%d_%d" % (u, c0))
-            nc.sync.dma_start(raw[:], x_rows[:, u, :, c0:c1])
-            return raw
-
         def load_w(w, j0, j1, name):
             raw = keep.tile([P, j1 - j0, H], F32, name="%s_raw_%d" % (name, j0))
             nc.sync.dma_start(raw[:], w.rearrange("(p j) c -> p j c", j=PACK)[:, j0:j1, :])
             return raw
 
+        def weave(target, source, copy):
+            copy(target.rearrange("p (c i) t -> p c t i", i=4), source.rearrange("p t (c i) -> p c t i", i=4))
+
+        def relu(target, source):
+            nc.scalar.activation(target, source, RELU)
+
+        def deal_w(raw, j0, dealt, t0, copy, m0=0, m1=P):
+            copy(
+                dealt[:, :, m0:m1, j0 : j0 + raw.shape[1]].rearrange("p t m j -> p m j t"),
+                raw[:].rearrange("p j (m t) -> p m j t", t=PACK)[:, m0:m1, :, t0 : t0 + dealt.shape[1]],
+            )
+
+        def quantize(codes, plane, c0, values):
+            cols = slice(c0, c0 + values.shape[1] // PACK)
+            nc.vector.quantize_mx(out=codes[:, cols].bitcast(FP8X4), scales=plane[:, cols], in_=values)
+
+        def quantize_w(dealt, i0, i1, codes, plane, t0):
+            quantize(codes, plane, t0 * P, dealt[:, i0:i1, :, :].rearrange("p t m j -> p (t m j)"))
+
+        def larger(target, a, b):
+            nc.vector.tensor_tensor(target, a, b, MAX)
+
+        x_rows = xT.rearrange("(p u e) c -> p u e c", u=2, e=2)
+
+        def load_pair(u, c0, c1):
+            raw = keep.tile([P, 2, c1 - c0], F32, name="x_raw_%d_%d" % (u, c0))
+            nc.sync.dma_start(raw[:], x_rows[:, u, :, c0:c1])
+            return raw
+
         x_chunks = [(0, 0, 1024), (1, 0, 512), (1, 512, 1024)]
-        x_raw = [load_x(*x_chunks[0])]
+        x_raw = [load_pair(*x_chunks[0])]
         offs_sb = load_list(offs, "offs_sb")
-        x_raw.extend(load_x(*chunk) for chunk in x_chunks[1:])
+        x_raw.extend(load_pair(*chunk) for chunk in x_chunks[1:])
+        w1_raw = [load_w(w1, 2 * u, 2 * u + 2, "w1") for u in range(2)]
         w2_raw = [load_w(w2, 2 * u, 2 * u + 2, "w2") for u in range(2)]
-        pos_sb = [load_list(pos, "pos_sb_%d" % d) for d, pos in enumerate((pos1, pos2, pos3, pos4))]
-        w1_raw = load_w(w1, 0, PACK, "w1")
         cen_sb = load_list(cen, "cen_sb")
+        pos_sb = [load_list(pos, "pos_sb_%d" % d) for d, pos in enumerate((pos1, pos2, pos3, pos4))]
 
         w3_codes = keep.tile([P, N], U32, align_bytes=64)
         nc.sync.dma_start(w3_codes[:].bitcast(I32), w3_words[0].rearrange("p n t -> p (n t)").bitcast(I32))
         w3_plane = keep.tile([P, N], U8, align_bytes=64)
-        nc.gpsimd.memset(w3_plane[:], 0)
+        nc.vector.memset(w3_plane[:].bitcast(I32), 0)
         for q in range(4):
             nc.sync.dma_start(w3_plane[32 * q : 32 * q + 4, :].bitcast(I32), w3_scales[0, 4 * q : 4 * q + 4, :].bitcast(I32))
 
@@ -67,39 +89,6 @@ def tile_picked_edgecv_relu_e_kernel(
         x_picked = [keep.tile([P, HALF_S, 2], U32, name="x_picked_%d" % h, align_bytes=64) for h in range(2)]
         x_codes = keep.tile([P, S], U32, align_bytes=64)
         x_plane = keep.tile([P, S], U8, align_bytes=64)
-
-        def pair_x(index, c0, c1, copy):
-            u, base = x_chunks[index][0:2]
-            copy(
-                x_pairs[u][:, base + c0 : base + c1, :].rearrange("p (c i) e -> p c e i", i=4),
-                x_raw[index][:, :, c0:c1].rearrange("p e (c i) -> p c e i", i=4),
-            )
-
-        def pick_x(u, h):
-            window = x_pairs[u][:].rearrange("p c e -> p (c e)").bitcast(U32)
-            nc.vector.tensor_copy(x_picked[h][:, :, u], window.indirect(offs_sb[:, 16 * h : 16 * (h + 1)]))
-
-        def quantize_x(h):
-            cols = slice(h * HALF_S, (h + 1) * HALF_S)
-            nc.vector.quantize_mx(
-                out=x_codes[:, cols].bitcast(FP8X4),
-                scales=x_plane[:, cols],
-                in_=x_picked[h][:].rearrange("p c u -> p (c u)").bitcast(BF16),
-            )
-
-        def deal_w(raw, j0, dealt, t0, t1, m0, m1, copy):
-            copy(
-                dealt[:, :, m0:m1, j0 : j0 + raw.shape[1]].rearrange("p t m j -> p m j t"),
-                raw[:].rearrange("p j (m t) -> p m j t", t=PACK)[:, m0:m1, :, t0:t1],
-            )
-
-        def quantize_w(dealt, codes, plane, t0, t1):
-            cols = slice(t0 * P, t1 * P)
-            nc.vector.quantize_mx(
-                out=codes[:, cols].bitcast(FP8X4),
-                scales=plane[:, cols],
-                in_=dealt.rearrange("p t m j -> p (t m j)"),
-            )
 
         def product(acc, codes, plane, t, cols):
             nc.tensor.matmul_mx(
@@ -112,10 +101,21 @@ def tile_picked_edgecv_relu_e_kernel(
                 stop=True,
             )
 
-        w2_codes = keep.tile([P, H], U32, align_bytes=64)
-        w2_plane = keep.tile([P, H], U8, align_bytes=64)
-        w1_codes = keep.tile([P, H], U32, align_bytes=64)
-        w1_plane = keep.tile([P, H], U8, align_bytes=64)
+        def whole_product(rows, codes, plane, t, bank="acc", bufs=3):
+            acc = psum.tile([P, S], F32, name=bank, bufs=bufs)
+            product(acc[:], codes, plane, t, slice(0, S))
+            nc.scalar.copy(rows[t][:], acc[:])
+
+        def quantize_x(h):
+            quantize(x_codes, x_plane, h * HALF_S, x_picked[h][:].rearrange("p c u -> p (c u)").bitcast(BF16))
+
+        def pair_x(index, c0, c1, copy):
+            u, base = x_chunks[index][0:2]
+            weave(x_pairs[u][:, base + c0 : base + c1, :], x_raw[index][:, :, c0:c1], copy)
+
+        def pick_x(u, h):
+            window = x_pairs[u][:].rearrange("p c e -> p (c e)").bitcast(U32)
+            nc.vector.tensor_copy(x_picked[h][:, :, u], window.indirect(offs_sb[:, 16 * h : 16 * (h + 1)]))
 
         pair_x(0, 0, 640, nc.vector.tensor_copy)
         pair_x(0, 640, 1024, nc.scalar.copy)
@@ -126,116 +126,85 @@ def tile_picked_edgecv_relu_e_kernel(
         pair_x(2, 352, 512, nc.scalar.copy)
         pick_x(1, 0)
         pick_x(1, 1)
-        quantize_x(0)
-        quantize_x(1)
 
-        w2_first = keep.tile([P, 1, P, PACK], BF16, tag="w2_dealt", align_bytes=64)
-        w2_last = keep.tile([P, 2, P, PACK], BF16, align_bytes=64)
-        for u in range(2):
-            deal_w(w2_raw[u], 2 * u, w2_first, 0, 1, 0, P, nc.scalar.copy)
-        deal_w(w2_raw[0], 0, w2_last, 2, 4, 0, 64, nc.scalar.copy)
-        deal_w(w2_raw[0], 0, w2_last, 2, 4, 64, P, nc.scalar.copy)
-        deal_w(w2_raw[1], 2, w2_last, 2, 4, 0, P, nc.scalar.copy)
-        quantize_w(w2_first[:], w2_codes, w2_plane, 0, 1)
-        w2_middle = keep.tile([P, 1, P, PACK], BF16, tag="w2_dealt", align_bytes=64)
-        for u in range(2):
-            deal_w(w2_raw[u], 2 * u, w2_middle, 1, 2, 0, P, nc.vector.tensor_copy)
-
+        w1_codes = keep.tile([P, H], U32, align_bytes=64)
+        w1_plane = keep.tile([P, H], U8, align_bytes=64)
+        w2_codes = keep.tile([P, H], U32, align_bytes=64)
+        w2_plane = keep.tile([P, H], U8, align_bytes=64)
         e_rows = [keep.tile([P, S], F32, name="e_rows_%d" % t) for t in range(PACK)]
-        y_rows = [keep.tile([P, S], F32, name="y_rows_%d" % t) for t in range(PACK)]
+        y_rows = [keep.tile([P, S], F32, name="y_rows_%d" % t, tag="y_rows_%d" % t, align_bytes=64) for t in range(PACK)]
 
-        for h, copy in enumerate((nc.scalar.copy, nc.vector.tensor_copy)):
-            cols = slice(h * HALF_S, (h + 1) * HALF_S)
-            acc_half = psum.tile([P, HALF_S], F32, name="acc_half", bufs=2)
-            product(acc_half[:], w2_codes, w2_plane, 0, cols)
-            copy(e_rows[0][:, cols], acc_half[:])
-
-
-        quantize_w(w2_middle[:], w2_codes, w2_plane, 1, 2)
-        quantize_w(w2_last[:], w2_codes, w2_plane, 2, 4)
-        for t in range(1, PACK):
-            acc = psum.tile([P, S], F32, name="acc", bufs=4)
-            product(acc[:], w2_codes, w2_plane, t, slice(0, S))
-            nc.scalar.copy(e_rows[t][:], acc[:])
-
-        w1_high = keep.tile([P, 2, P, PACK], BF16, tag="w1_high", align_bytes=64)
-        w1_low = keep.tile([P, 2, P, PACK], BF16, align_bytes=64)
-        for dealt, t0 in ((w1_high, 2), (w1_low, 0)):
-            for m0 in (0, 64):
-                deal_w(w1_raw, 0, dealt, t0, t0 + 2, m0, m0 + 64, nc.scalar.copy)
-
-        fetched = keep.tile([P, 4, V], F32)
-        early = keep.tile([P, 2, V], F32)
-        pair_max = [keep.tile([P, 2, V], F32, name="pair_max_%d" % t) for t in range(2)]
-        largest = keep.tile([P, 2, V], F32)
-        summed = keep.tile([P, 2, V], F32)
-        centre = {t: keep.tile([P, V], F32, name="centre_%d" % t) for t in (2, 3)}
-        edge = [keep.tile([P, 2, V], F32, name="edge_%d" % d) for d in range(3)]
-        high = [keep.tile([P, V, 2], BF16, name="high_%d" % d) for d in range(3)]
-        high_max = [keep.tile([P, V, 2], BF16, name="high_max_%d" % d) for d in range(2)]
-        z_woven = [keep.tile([P, HALF_V, PACK], BF16, name="z_woven_%d" % h, align_bytes=64) for h in range(2)]
-
-        def whole_product(rows, codes, plane, t):
-            acc = psum.tile([P, S], F32, name="acc", bufs=4)
-            product(acc[:], codes, plane, t, slice(0, S))
-            nc.scalar.copy(rows[t][:], acc[:])
-
-        def fetch(target, t, d):
-            nc.vector.tensor_copy(target, e_rows[t][:].indirect(pos_sb[d][:]))
+        def fetch_centre(t):
+            nc.vector.tensor_copy(centre[:, t, :], y_rows[t][:].indirect(cen_sb[:]))
 
         def fetch_edge(target, t, d, v0, v1):
-            nc.vector.tensor_tensor(target, e_rows[t][:].indirect(pos_sb[d][:, v0 // 16 : v1 // 16]), centre[t][:, v0:v1], ADD)
+            nc.vector.tensor_tensor(target, e_rows[t][:].indirect(pos_sb[d][:, v0 // 16 : v1 // 16]), centre[:, t, v0:v1], ADD)
 
-        def weave(target, source):
-            nc.scalar.activation(
-                target.rearrange("p (c i) t -> p c t i", i=4), source.rearrange("p t (c i) -> p c t i", i=4), RELU
-            )
-
-        def larger(target, a, b):
-            nc.vector.tensor_tensor(target, a, b, MAX)
-
-        for d in range(4):
-            fetch(fetched[:, d, :], 0, d)
-        fetch(early[:, 0, :], 1, 0)
-        larger(pair_max[0][:], fetched[:, 0:2, :], fetched[:, 2:4, :])
-        fetch(early[:, 1, :], 1, 1)
-        quantize_w(w1_high[:], w1_codes, w1_plane, 2, 4)
-        larger(largest[:, 0, :], pair_max[0][:, 0, :], pair_max[0][:, 1, :])
-        for t in (2, 3):
-            whole_product(y_rows, w1_codes, w1_plane, t)
-        late = keep.tile([P, 2, V], F32, tag="w1_high", align_bytes=64)
-        fetch(late[:, 0, :], 1, 2)
-        fetch(late[:, 1, :], 1, 3)
-        quantize_w(w1_low[:], w1_codes, w1_plane, 0, 2)
-        larger(pair_max[1][:], early[:], late[:])
+        w1_low = keep.tile([P, 2, P, PACK], BF16, align_bytes=64)
+        w1_high = keep.tile([P, 2, P, PACK], BF16, align_bytes=64)
+        deal_w(w1_raw[0], 0, w1_low, 0, nc.scalar.copy)
+        deal_w(w1_raw[0], 0, w1_high, 2, nc.scalar.copy)
+        deal_w(w1_raw[1], 2, w1_high, 2, nc.scalar.copy)
+        quantize_x(0)
+        deal_w(w1_raw[1], 2, w1_low, 0, nc.vector.tensor_copy)
+        quantize_x(1)
+        quantize_w(w1_low, 0, 1, w1_codes, w1_plane, 0)
+        quantize_w(w1_low, 1, 2, w1_codes, w1_plane, 1)
+        quantize_w(w1_high, 0, 2, w1_codes, w1_plane, 2)
+        w2_low = keep.tile([P, 2, P, PACK], BF16, tag="w2_low", align_bytes=64)
+        for u in range(2):
+            deal_w(w2_raw[u], 2 * u, w2_low, 0, nc.vector.tensor_copy)
+        quantize_w(w2_low, 0, 2, w2_codes, w2_plane, 0)
+        for t in range(PACK):
+            whole_product(y_rows, w1_codes, w1_plane, t, "acc", 6)
         for t in range(2):
-            whole_product(y_rows, w1_codes, w1_plane, t)
-        nc.vector.tensor_copy(centre[2][:], y_rows[2][:].indirect(cen_sb[:]))
-        larger(largest[:, 1, :], pair_max[1][:, 0, :], pair_max[1][:, 1, :])
-        nc.vector.tensor_copy(centre[3][:], y_rows[3][:].indirect(cen_sb[:]))
+            whole_product(e_rows, w2_codes, w2_plane, t, "acc", 6)
+        centre = keep.tile([P, PACK, V], F32, tag="w2_low", align_bytes=64)
+        for t in range(PACK):
+            fetch_centre(t)
+        w2_high = keep.tile([P, 2, P, PACK], BF16, tag="y_rows_3", align_bytes=64)
+        for u in range(2):
+            deal_w(w2_raw[u], 2 * u, w2_high, 2, nc.scalar.copy)
+
+        woven = [keep.tile([P, V, PACK], BF16, name="woven_%d" % d) for d in range(3)]
+        last = [keep.tile([P, HALF_V, PACK], BF16, name="last_%d" % h) for h in range(2)]
+        first_max = keep.tile([P, V, PACK], BF16)
+        second_max = [keep.tile([P, HALF_V, PACK], BF16, name="second_max_%d" % h) for h in range(2)]
+        low_edge = [keep.tile([P, 2, V], F32, name="low_edge_%d" % d) for d in range(2)]
+        high_edge = [keep.tile([P, 2, V], F32, name="high_edge_%d" % d) for d in range(3)]
+
+        for d in range(2):
+            for t in range(2):
+                fetch_edge(low_edge[d][:, t, :], t, d, 0, V)
+        quantize_w(w2_high, 0, 2, w2_codes, w2_plane, 2)
+        for t in (2, 3):
+            whole_product(e_rows, w2_codes, w2_plane, t, "acc", 6)
+        for d in range(2):
+            weave(woven[d][:, :, 0:2], low_edge[d][:], relu)
+        late_edge = keep.tile([P, 2, 2, V], F32, tag="y_rows_3", align_bytes=64)
+        for d in (2, 3):
+            for t in range(2):
+                fetch_edge(late_edge[:, d - 2, t, :], t, d, 0, V)
+        weave(woven[2][:, :, 0:2], late_edge[:, 0, :, :], relu)
+        for h in range(2):
+            weave(last[h][:, :, 0:2], late_edge[:, 1, :, h * HALF_V : (h + 1) * HALF_V], relu)
         for d in range(3):
             for t in (2, 3):
-                fetch_edge(edge[d][:, t - 2, :], t, d, 0, V)
-            weave(high[d][:], edge[d][:])
-        for t in range(2):
-            nc.vector.tensor_tensor(summed[:, t, :], y_rows[t][:].indirect(cen_sb[:]), largest[:, t, :], ADD)
-        for h in range(2):
-            weave(z_woven[h][:, :, 0:2], summed[:, :, h * HALF_V : (h + 1) * HALF_V])
+                fetch_edge(high_edge[d][:, t - 2, :], t, d, 0, V)
+            weave(woven[d][:, :, 2:4], high_edge[d][:], relu)
+        last_edge = [keep.tile([P, 2, HALF_V], F32, name="last_edge_%d" % h) for h in range(2)]
 
-        def last_edge(t, h):
-            fetch_edge(edge[1 + h][:, t - 2, 0:HALF_V], t, 3, h * HALF_V, (h + 1) * HALF_V)
-
-        def finish_z(h):
-            larger(
-                z_woven[h][:, :, 2:4].rearrange("p (c i) t -> p c t i", i=4),
-                edge[1 + h][:, :, 0:HALF_V].rearrange("p t (c i) -> p c t i", i=4),
-                high_max[1][:, h * HALF_V : (h + 1) * HALF_V, :].rearrange("p (c i) t -> p c t i", i=4),
-            )
+        def fetch_last(h):
+            for t in (2, 3):
+                fetch_edge(last_edge[h][:, t - 2, :], t, 3, h * HALF_V, (h + 1) * HALF_V)
+            weave(last[h][:, :, 2:4], last_edge[h][:], relu)
 
         def project(h):
+            z_woven = keep.tile([P, HALF_V, PACK], BF16, name="z_woven_%d" % h, align_bytes=64)
+            larger(z_woven[:], first_max[:, h * HALF_V : (h + 1) * HALF_V, :], second_max[h][:])
             z_codes = keep.tile([P, HALF_V], U32, name="z_codes_%d" % h, align_bytes=64)
             z_plane = keep.tile([P, HALF_V], U8, name="z_plane_%d" % h, align_bytes=64)
-            nc.vector.quantize_mx(out=z_codes[:].bitcast(FP8X4), scales=z_plane[:], in_=z_woven[h][:].rearrange("p v t -> p (v t)"))
+            quantize(z_codes, z_plane, 0, z_woven[:].rearrange("p v t -> p (v t)"))
             acc_out = psum.tile([P, HALF_V], F32, name="acc_out", bufs=2)
             nc.tensor.matmul_mx(
                 out=acc_out[:],
@@ -250,13 +219,10 @@ def tile_picked_edgecv_relu_e_kernel(
             nc.scalar.copy(result[:], acc_out[:])
             nc.sync.dma_start(out[:, h * HALF_V : (h + 1) * HALF_V], result[:])
 
-        larger(high_max[0][:], high[0][:], high[1][:])
-        last_edge(2, 0)
-        last_edge(3, 0)
-        larger(high_max[1][:], high_max[0][:], high[2][:])
-        last_edge(2, 1)
-        finish_z(0)
-        last_edge(3, 1)
+        fetch_last(0)
+        fetch_last(1)
+        larger(first_max[:], woven[0][:], woven[1][:])
+        for h in range(2):
+            larger(second_max[h][:], woven[2][:, h * HALF_V : (h + 1) * HALF_V, :], last[h][:])
         project(0)
-        finish_z(1)
         project(1)

@@ -48,8 +48,8 @@ def tile_picked_edgecv_relu_e_kernel(
 
         def deal_w(raw, j0, dealt, t0, copy, m0=0, m1=P):
             copy(
-                dealt[:, :, m0:m1, j0 : j0 + raw.shape[1]].rearrange("p t m j -> p m j t"),
-                raw[:].rearrange("p j (m t) -> p m j t", t=PACK)[:, m0:m1, :, t0 : t0 + dealt.shape[1]],
+                dealt[:, :, m0:m1, j0 : j0 + raw.shape[1]].rearrange("p t (c i) j -> p c t i j", i=2),
+                raw[:].rearrange("p j (c i t) -> p c t i j", i=2, t=PACK)[:, m0 // 2 : m1 // 2, t0 : t0 + dealt.shape[1], :, :],
             )
 
         def quantize(codes, plane, c0, values):
@@ -166,10 +166,10 @@ def tile_picked_edgecv_relu_e_kernel(
         for u in range(2):
             deal_w(w2_raw[u], 2 * u, w2_high, 2, nc.scalar.copy)
 
-        woven = [keep.tile([P, V, PACK], BF16, name="woven_%d" % d) for d in range(3)]
-        last = [keep.tile([P, HALF_V, PACK], BF16, name="last_%d" % h) for h in range(2)]
-        first_max = keep.tile([P, V, PACK], BF16)
-        second_max = [keep.tile([P, HALF_V, PACK], BF16, name="second_max_%d" % h) for h in range(2)]
+        woven = [keep.tile([P, 2, V, 2], BF16, name="woven_%d" % d) for d in range(3)]
+        last = [keep.tile([P, 2, HALF_V, 2], BF16, name="last_%d" % h) for h in range(2)]
+        first_max = keep.tile([P, 2, V, 2], BF16)
+        second_max = [keep.tile([P, 2, HALF_V, 2], BF16, name="second_max_%d" % h) for h in range(2)]
         low_edge = [keep.tile([P, 2, V], F32, name="low_edge_%d" % d) for d in range(2)]
         high_edge = [keep.tile([P, 2, V], F32, name="high_edge_%d" % d) for d in range(3)]
 
@@ -180,28 +180,32 @@ def tile_picked_edgecv_relu_e_kernel(
         for t in (2, 3):
             whole_product(e_rows, w2_codes, w2_plane, t, "acc", 6)
         for d in range(2):
-            weave(woven[d][:, :, 0:2], low_edge[d][:], relu)
+            weave(woven[d][:, 0, :, :], low_edge[d][:], relu)
         late_edge = keep.tile([P, 2, 2, V], F32, tag="y_rows_3", align_bytes=64)
         for d in (2, 3):
             for t in range(2):
                 fetch_edge(late_edge[:, d - 2, t, :], t, d, 0, V)
-        weave(woven[2][:, :, 0:2], late_edge[:, 0, :, :], relu)
+        weave(woven[2][:, 0, :, :], late_edge[:, 0, :, :], relu)
         for h in range(2):
-            weave(last[h][:, :, 0:2], late_edge[:, 1, :, h * HALF_V : (h + 1) * HALF_V], relu)
+            weave(last[h][:, 0, :, :], late_edge[:, 1, :, h * HALF_V : (h + 1) * HALF_V], relu)
         for d in range(3):
             for t in (2, 3):
                 fetch_edge(high_edge[d][:, t - 2, :], t, d, 0, V)
-            weave(woven[d][:, :, 2:4], high_edge[d][:], relu)
+            weave(woven[d][:, 1, :, :], high_edge[d][:], relu)
         last_edge = [keep.tile([P, 2, HALF_V], F32, name="last_edge_%d" % h) for h in range(2)]
 
         def fetch_last(h):
             for t in (2, 3):
                 fetch_edge(last_edge[h][:, t - 2, :], t, 3, h * HALF_V, (h + 1) * HALF_V)
-            weave(last[h][:, :, 2:4], last_edge[h][:], relu)
+            weave(last[h][:, 1, :, :], last_edge[h][:], relu)
 
         def project(h):
             z_woven = keep.tile([P, HALF_V, PACK], BF16, name="z_woven_%d" % h, align_bytes=64)
-            larger(z_woven[:], first_max[:, h * HALF_V : (h + 1) * HALF_V, :], second_max[h][:])
+            larger(
+                z_woven[:].rearrange("p v (g e) -> p v g e", g=2),
+                first_max[:, :, h * HALF_V : (h + 1) * HALF_V, :].rearrange("p g v e -> p v g e"),
+                second_max[h][:].rearrange("p g v e -> p v g e"),
+            )
             z_codes = keep.tile([P, HALF_V], U32, name="z_codes_%d" % h, align_bytes=64)
             z_plane = keep.tile([P, HALF_V], U8, name="z_plane_%d" % h, align_bytes=64)
             quantize(z_codes, z_plane, 0, z_woven[:].rearrange("p v t -> p (v t)"))
@@ -223,6 +227,6 @@ def tile_picked_edgecv_relu_e_kernel(
         fetch_last(1)
         larger(first_max[:], woven[0][:], woven[1][:])
         for h in range(2):
-            larger(second_max[h][:], woven[2][:, h * HALF_V : (h + 1) * HALF_V, :], last[h][:])
+            larger(second_max[h][:], woven[2][:, :, h * HALF_V : (h + 1) * HALF_V, :], last[h][:])
         project(0)
         project(1)

@@ -48,7 +48,7 @@ def tile_picked_edgecv_relu_e_kernel(
 
         def deal_w(raw, j0, dealt, t0, copy, m0=0, m1=P):
             copy(
-                dealt[:, :, m0:m1, j0 : j0 + raw.shape[1]].rearrange("p t (c i) j -> p c t i j", i=2),
+                dealt[:, :, :, j0 : j0 + raw.shape[1]].rearrange("p t (c i) j -> p c t i j", i=2),
                 raw[:].rearrange("p j (c i t) -> p c t i j", i=2, t=PACK)[:, m0 // 2 : m1 // 2, t0 : t0 + dealt.shape[1], :, :],
             )
 
@@ -58,6 +58,9 @@ def tile_picked_edgecv_relu_e_kernel(
 
         def quantize_w(dealt, i0, i1, codes, plane, t0):
             quantize(codes, plane, t0 * P, dealt[:, i0:i1, :, :].rearrange("p t m j -> p (t m j)"))
+
+        def quantize_part(dealt, t, m0, codes, plane):
+            quantize(codes, plane, t * P + m0, dealt[:, t, :, :].rearrange("p m j -> p (m j)"))
 
         def larger(target, a, b):
             nc.vector.tensor_tensor(target, a, b, MAX)
@@ -140,26 +143,32 @@ def tile_picked_edgecv_relu_e_kernel(
         def fetch_edge(target, t, d, v0, v1):
             nc.vector.tensor_tensor(target, e_rows[t][:].indirect(pos_sb[d][:, v0 // 16 : v1 // 16]), centre[:, t, v0:v1], ADD)
 
-        w1_low = keep.tile([P, 2, P, PACK], BF16, align_bytes=64)
+        w1_low = [keep.tile([P, 2, 64, PACK], BF16, name="w1_low_%d" % g, align_bytes=64) for g in range(2)]
         w1_high = keep.tile([P, 2, P, PACK], BF16, align_bytes=64)
-        deal_w(w1_raw[0], 0, w1_low, 0, nc.scalar.copy)
+        for g in range(2):
+            deal_w(w1_raw[0], 0, w1_low[g], 0, nc.scalar.copy, 64 * g, 64 * g + 64)
         deal_w(w1_raw[0], 0, w1_high, 2, nc.scalar.copy)
         deal_w(w1_raw[1], 2, w1_high, 2, nc.scalar.copy)
         quantize_x(0)
-        deal_w(w1_raw[1], 2, w1_low, 0, nc.vector.tensor_copy)
         quantize_x(1)
-        quantize_w(w1_low, 0, 1, w1_codes, w1_plane, 0)
-        quantize_w(w1_low, 1, 2, w1_codes, w1_plane, 1)
+        for g in range(2):
+            deal_w(w1_raw[1], 2, w1_low[g], 0, nc.vector.tensor_copy, 64 * g, 64 * g + 64)
+        for t in range(2):
+            for g in range(2):
+                quantize_part(w1_low[g], t, 64 * g, w1_codes, w1_plane)
         quantize_w(w1_high, 0, 2, w1_codes, w1_plane, 2)
-        w2_low = keep.tile([P, 2, P, PACK], BF16, tag="w2_low", align_bytes=64)
+        w2_low = [keep.tile([P, 2, 64, PACK], BF16, name="w2_low_%d" % g, tag="w2_low_%d" % g, align_bytes=64) for g in range(2)]
         for u in range(2):
-            deal_w(w2_raw[u], 2 * u, w2_low, 0, nc.vector.tensor_copy)
-        quantize_w(w2_low, 0, 2, w2_codes, w2_plane, 0)
+            for g in range(2):
+                deal_w(w2_raw[u], 2 * u, w2_low[g], 0, nc.vector.tensor_copy, 64 * g, 64 * g + 64)
+        for g in range(2):
+            for t in range(2):
+                quantize_part(w2_low[g], t, 64 * g, w2_codes, w2_plane)
         for t in range(PACK):
             whole_product(y_rows, w1_codes, w1_plane, t, "acc", 6)
         for t in range(2):
             whole_product(e_rows, w2_codes, w2_plane, t, "acc", 6)
-        centre = keep.tile([P, PACK, V], F32, tag="w2_low", align_bytes=64)
+        centre = keep.tile([P, PACK, V], F32, tag="w2_low_1", align_bytes=64)
         for t in range(PACK):
             fetch_centre(t)
         w2_high = keep.tile([P, 2, P, PACK], BF16, tag="y_rows_3", align_bytes=64)

@@ -125,8 +125,8 @@ def tile_picked_edgecv_relu_e_kernel(
         pick_x(0, 0)
         pick_x(0, 1)
         pair_x(1, 0, 512, nc.scalar.copy)
-        pair_x(2, 0, 352, nc.vector.tensor_copy)
-        pair_x(2, 352, 512, nc.scalar.copy)
+        pair_x(2, 0, 288, nc.vector.tensor_copy)
+        pair_x(2, 288, 512, nc.scalar.copy)
         pick_x(1, 0)
         pick_x(1, 1)
 
@@ -135,7 +135,9 @@ def tile_picked_edgecv_relu_e_kernel(
         w2_codes = keep.tile([P, H], U32, align_bytes=64)
         w2_plane = keep.tile([P, H], U8, align_bytes=64)
         e_rows = [keep.tile([P, S], F32, name="e_rows_%d" % t) for t in range(PACK)]
-        y_rows = [keep.tile([P, S], F32, name="y_rows_%d" % t, tag="y_rows_%d" % t, align_bytes=64) for t in range(PACK)]
+        held = ctx.enter_context(tc.tile_pool(name="held", bufs=1))
+        y_rows = [keep.tile([P, S], F32, name="y_rows_%d" % t) for t in range(PACK - 1)]
+        y_rows.append(held.tile([P, S], F32, name="y_rows_3", offset=3072, align_bytes=64))
 
         def fetch_centre(t):
             nc.vector.tensor_copy(centre[:, t, :], y_rows[t][:].indirect(cen_sb[:]))
@@ -153,8 +155,8 @@ def tile_picked_edgecv_relu_e_kernel(
         quantize_x(1)
         for g in range(2):
             deal_w(w1_raw[1], 2, w1_low[g], 0, nc.vector.tensor_copy, 64 * g, 64 * g + 64)
-        for t in range(2):
-            for g in range(2):
+        for g in range(2):
+            for t in range(2):
                 quantize_part(w1_low[g], t, 64 * g, w1_codes, w1_plane)
         quantize_w(w1_high, 0, 2, w1_codes, w1_plane, 2)
         w2_low = [keep.tile([P, 2, 64, PACK], BF16, name="w2_low_%d" % g, tag="w2_low_%d" % g, align_bytes=64) for g in range(2)]
@@ -168,12 +170,13 @@ def tile_picked_edgecv_relu_e_kernel(
             whole_product(y_rows, w1_codes, w1_plane, t, "acc", 6)
         for t in range(2):
             whole_product(e_rows, w2_codes, w2_plane, t, "acc", 6)
-        centre = keep.tile([P, PACK, V], F32, tag="w2_low_1", align_bytes=64)
+        centre = keep.tile([P, PACK, V], F32, tag="w2_low_0", align_bytes=64)
         for t in range(PACK):
             fetch_centre(t)
-        w2_high = keep.tile([P, 2, P, PACK], BF16, tag="y_rows_3", align_bytes=64)
+        w2_high = [held.tile([P, 2, 64, PACK], BF16, name="w2_high_%d" % g, offset=3072 + 1024 * g, align_bytes=64) for g in range(2)]
         for u in range(2):
-            deal_w(w2_raw[u], 2 * u, w2_high, 2, nc.scalar.copy)
+            for g in range(2):
+                deal_w(w2_raw[u], 2 * u, w2_high[g], 2, nc.scalar.copy, 64 * g, 64 * g + 64)
 
         woven = [keep.tile([P, 2, V, 2], BF16, name="woven_%d" % d) for d in range(3)]
         last = [keep.tile([P, 2, HALF_V, 2], BF16, name="last_%d" % h) for h in range(2)]
@@ -185,12 +188,14 @@ def tile_picked_edgecv_relu_e_kernel(
         for d in range(2):
             for t in range(2):
                 fetch_edge(low_edge[d][:, t, :], t, d, 0, V)
-        quantize_w(w2_high, 0, 2, w2_codes, w2_plane, 2)
+        for g in range(2):
+            for t in range(2):
+                quantize_part(w2_high[g], t, 2 * P + 64 * g, w2_codes, w2_plane)
         for t in (2, 3):
             whole_product(e_rows, w2_codes, w2_plane, t, "acc", 6)
         for d in range(2):
             weave(woven[d][:, 0, :, :], low_edge[d][:], relu)
-        late_edge = keep.tile([P, 2, 2, V], F32, tag="y_rows_3", align_bytes=64)
+        late_edge = held.tile([P, 2, 2, V], F32, offset=0, align_bytes=64)
         for d in (2, 3):
             for t in range(2):
                 fetch_edge(late_edge[:, d - 2, t, :], t, d, 0, V)
@@ -230,7 +235,7 @@ def tile_picked_edgecv_relu_e_kernel(
             )
             result = keep.tile([P, HALF_V], F32, name="result_%d" % h)
             nc.scalar.copy(result[:], acc_out[:])
-            nc.sync.dma_start(out[:, h * HALF_V : (h + 1) * HALF_V], result[:])
+            (nc.sync, nc.scalar)[h].dma_start(out[:, h * HALF_V : (h + 1) * HALF_V], result[:])
 
         fetch_last(0)
         fetch_last(1)

@@ -105,7 +105,7 @@ def tile_picked_edgecv_relu_e_kernel(
             )
 
         def whole_product(rows, codes, plane, t, bank="acc", bufs=3):
-            acc = psum.tile([P, S], F32, name=bank, bufs=bufs)
+            acc = psum.tile([P, S], F32, name=bank, tag=bank, bufs=bufs)
             product(acc[:], codes, plane, t, slice(0, S))
             nc.scalar.copy(rows[t][:], acc[:])
 
@@ -166,7 +166,12 @@ def tile_picked_edgecv_relu_e_kernel(
         for g in range(2):
             for t in range(2):
                 quantize_part(w2_low[g], t, 64 * g, w2_codes, w2_plane)
-        for t in range(PACK):
+        for h in range(PACK):
+            cols = slice(h * P, (h + 1) * P)
+            acc_half = psum.tile([P, P], F32, name="acc_half", tag="acc", bufs=6)
+            product(acc_half[:], w1_codes, w1_plane, 0, cols)
+            nc.scalar.copy(y_rows[0][:, cols], acc_half[:])
+        for t in range(1, PACK):
             whole_product(y_rows, w1_codes, w1_plane, t, "acc", 6)
         for t in range(2):
             whole_product(e_rows, w2_codes, w2_plane, t, "acc", 6)
@@ -179,9 +184,10 @@ def tile_picked_edgecv_relu_e_kernel(
                 deal_w(w2_raw[u], 2 * u, w2_high[g], 2, nc.scalar.copy, 64 * g, 64 * g + 64)
 
         woven = [keep.tile([P, 2, V, 2], BF16, name="woven_%d" % d) for d in range(3)]
-        last = [keep.tile([P, 2, HALF_V, 2], BF16, name="last_%d" % h) for h in range(2)]
+        pieces = [(0, 128), (128, 192), (192, 256)]
+        last = [keep.tile([P, 2, v1 - v0, 2], BF16, name="last_%d" % v0) for v0, v1 in pieces]
         first_max = keep.tile([P, 2, V, 2], BF16)
-        second_max = [keep.tile([P, 2, HALF_V, 2], BF16, name="second_max_%d" % h) for h in range(2)]
+        second_max = [keep.tile([P, 2, v1 - v0, 2], BF16, name="second_max_%d" % v0) for v0, v1 in pieces]
         low_edge = [keep.tile([P, 2, V], F32, name="low_edge_%d" % d) for d in range(2)]
         high_edge = [keep.tile([P, 2, V], F32, name="high_edge_%d" % d) for d in range(3)]
 
@@ -200,8 +206,8 @@ def tile_picked_edgecv_relu_e_kernel(
             for t in range(2):
                 fetch_edge(late_edge[:, d - 2, t, :], t, d, 0, V)
         weave(woven[2][:, 0, :, :], late_edge[:, 0, :, :], relu)
-        for h in range(2):
-            weave(last[h][:, 0, :, :], late_edge[:, 1, :, h * HALF_V : (h + 1) * HALF_V], relu)
+        for h, (v0, v1) in enumerate(pieces):
+            weave(last[h][:, 0, :, :], late_edge[:, 1, :, v0:v1], relu)
         for d in range(3):
             for t in (2, 3):
                 fetch_edge(high_edge[d][:, t - 2, :], t, d, 0, V)
@@ -211,19 +217,22 @@ def tile_picked_edgecv_relu_e_kernel(
         def fetch_last(h):
             for t in (2, 3):
                 fetch_edge(last_edge[h][:, t - 2, :], t, 3, h * HALF_V, (h + 1) * HALF_V)
-            weave(last[h][:, 1, :, :], last_edge[h][:], relu)
+            for g, (v0, v1) in enumerate(pieces):
+                if v0 // HALF_V == h:
+                    weave(last[g][:, 1, :, :], last_edge[h][:, :, v0 - h * HALF_V : v1 - h * HALF_V], relu)
 
         def project(h):
-            z_woven = keep.tile([P, HALF_V, PACK], BF16, name="z_woven_%d" % h, align_bytes=64)
+            v0, v1 = pieces[h]
+            z_woven = keep.tile([P, v1 - v0, PACK], BF16, name="z_woven_%d" % h, align_bytes=64)
             larger(
                 z_woven[:].rearrange("p v (g e) -> p v g e", g=2),
-                first_max[:, :, h * HALF_V : (h + 1) * HALF_V, :].rearrange("p g v e -> p v g e"),
+                first_max[:, :, v0:v1, :].rearrange("p g v e -> p v g e"),
                 second_max[h][:].rearrange("p g v e -> p v g e"),
             )
-            z_codes = keep.tile([P, HALF_V], U32, name="z_codes_%d" % h, align_bytes=64)
-            z_plane = keep.tile([P, HALF_V], U8, name="z_plane_%d" % h, align_bytes=64)
+            z_codes = keep.tile([P, v1 - v0], U32, name="z_codes_%d" % h, align_bytes=64)
+            z_plane = keep.tile([P, v1 - v0], U8, name="z_plane_%d" % h, align_bytes=64)
             quantize(z_codes, z_plane, 0, z_woven[:].rearrange("p v t -> p (v t)"))
-            acc_out = psum.tile([P, HALF_V], F32, name="acc_out", bufs=2)
+            acc_out = psum.tile([P, v1 - v0], F32, name="acc_out", tag="acc", bufs=6)
             nc.tensor.matmul_mx(
                 out=acc_out[:],
                 lhsT=w3_codes[:].bitcast(FP8X4),
@@ -233,14 +242,15 @@ def tile_picked_edgecv_relu_e_kernel(
                 start=True,
                 stop=True,
             )
-            result = keep.tile([P, HALF_V], F32, name="result_%d" % h)
-            nc.scalar.copy(result[:], acc_out[:])
-            (nc.sync, nc.scalar)[h].dma_start(out[:, h * HALF_V : (h + 1) * HALF_V], result[:])
+            result = keep.tile([P, v1 - v0], F32, name="result_%d" % h)
+            (nc.scalar.copy, nc.scalar.copy, nc.vector.tensor_copy)[h](result[:], acc_out[:])
+            nc.sync.dma_start(out[:, v0:v1], result[:])
 
         fetch_last(0)
         fetch_last(1)
         larger(first_max[:], woven[0][:], woven[1][:])
-        for h in range(2):
-            larger(second_max[h][:], woven[2][:, :, h * HALF_V : (h + 1) * HALF_V, :], last[h][:])
+        for h, (v0, v1) in enumerate(pieces):
+            larger(second_max[h][:], woven[2][:, :, v0:v1, :], last[h][:])
         project(0)
         project(1)
+        project(2)

@@ -13,6 +13,7 @@ U16 = mybir.dt.uint16
 U8 = mybir.dt.uint8
 FP8X4 = mybir.dt.float8_e4m3fn_x4
 ADD = mybir.AluOpType.add
+MULT = mybir.AluOpType.mult
 MAX = mybir.AluOpType.max
 RELU = mybir.ActivationFunctionType.Relu
 
@@ -116,19 +117,25 @@ def tile_picked_edgecv_relu_e_kernel(
             u, base = x_chunks[index][0:2]
             weave(x_pairs[u][:, base + c0 : base + c1, :], x_raw[index][:, :, c0:c1], copy)
 
-        def pick_x(u, h):
+        x_rows_picked = keep.tile([P, 2, S], U32)
+
+        def pick_x(u, c0, c1):
             window = x_pairs[u][:].rearrange("p c e -> p (c e)").bitcast(U32)
-            nc.vector.tensor_copy(x_picked[h][:, :, u], window.indirect(offs_sb[:, 16 * h : 16 * (h + 1)]))
+            nc.vector.tensor_copy(x_rows_picked[:, u, c0:c1], window.indirect(offs_sb[:, c0 // 16 : c1 // 16]))
+
+        def join_x(h):
+            nc.vector.tensor_copy(x_picked[h][:].bitcast(I32), x_rows_picked[:, :, h * HALF_S : (h + 1) * HALF_S].bitcast(I32).rearrange("p u c -> p c u"))
 
         pair_x(0, 0, 640, nc.vector.tensor_copy)
         pair_x(0, 640, 1024, nc.scalar.copy)
-        pick_x(0, 0)
-        pick_x(0, 1)
+        pick_x(0, 0, S)
         pair_x(1, 0, 512, nc.scalar.copy)
-        pair_x(2, 0, 288, nc.vector.tensor_copy)
-        pair_x(2, 288, 512, nc.scalar.copy)
-        pick_x(1, 0)
-        pick_x(1, 1)
+        pair_x(2, 0, 352, nc.vector.tensor_copy)
+        pair_x(2, 352, 512, nc.scalar.copy)
+        pick_x(1, 0, HALF_S)
+        pick_x(1, HALF_S, S)
+        join_x(0)
+        join_x(1)
 
         w1_codes = keep.tile([P, H], U32, align_bytes=64)
         w1_plane = keep.tile([P, H], U8, align_bytes=64)
@@ -136,8 +143,17 @@ def tile_picked_edgecv_relu_e_kernel(
         w2_plane = keep.tile([P, H], U8, align_bytes=64)
         e_rows = [keep.tile([P, S], F32, name="e_rows_%d" % t) for t in range(PACK)]
         held = ctx.enter_context(tc.tile_pool(name="held", bufs=1))
-        y_rows = [keep.tile([P, S], F32, name="y_rows_%d" % t) for t in range(PACK - 1)]
-        y_rows.append(held.tile([P, S], F32, name="y_rows_3", offset=3072, align_bytes=64))
+        y_rows = [keep.tile([P, S], F32, name="y_rows_%d" % t) for t in range(PACK)]
+
+        def deal_high(raw, j0, dealt):
+            nc.gpsimd.tensor_scalar(
+                dealt[:, :, :, j0 : j0 + 2].rearrange("p t m j -> p m t j"),
+                raw[:].rearrange("p j (m t) -> p m t j", t=PACK)[:, :, 2:4, :],
+                1.0,
+                0.0,
+                MULT,
+                ADD,
+            )
 
         def fetch_centre(t):
             nc.vector.tensor_copy(centre[:, t, :], y_rows[t][:].indirect(cen_sb[:]))
@@ -145,24 +161,25 @@ def tile_picked_edgecv_relu_e_kernel(
         def fetch_edge(target, t, d, v0, v1):
             nc.vector.tensor_tensor(target, e_rows[t][:].indirect(pos_sb[d][:, v0 // 16 : v1 // 16]), centre[:, t, v0:v1], ADD)
 
-        w1_low = [keep.tile([P, 2, 64, PACK], BF16, name="w1_low_%d" % g, align_bytes=64) for g in range(2)]
+        w1_low = keep.tile([P, 2, P, PACK], BF16, align_bytes=64)
         w1_high = keep.tile([P, 2, P, PACK], BF16, align_bytes=64)
-        for g in range(2):
-            deal_w(w1_raw[0], 0, w1_low[g], 0, nc.scalar.copy, 64 * g, 64 * g + 64)
-        deal_w(w1_raw[0], 0, w1_high, 2, nc.scalar.copy)
+        deal_w(w1_raw[0], 0, w1_low, 0, nc.scalar.copy)
+        deal_high(w1_raw[0], 0, w1_high)
+        deal_w(w1_raw[1], 2, w1_low, 0, nc.scalar.copy)
         deal_w(w1_raw[1], 2, w1_high, 2, nc.scalar.copy)
         quantize_x(0)
         quantize_x(1)
+        for t in range(2):
+            quantize_w(w1_low, t, t + 1, w1_codes, w1_plane, t)
+        w2_low = [
+            keep.tile([P, 2, 64, PACK], BF16, name="w2_low_0", tag="w2_low_0", align_bytes=64),
+            held.tile([P, 2, 64, PACK], BF16, name="w2_low_1", offset=0, align_bytes=64),
+        ]
         for g in range(2):
-            deal_w(w1_raw[1], 2, w1_low[g], 0, nc.vector.tensor_copy, 64 * g, 64 * g + 64)
-        for g in range(2):
-            for t in range(2):
-                quantize_part(w1_low[g], t, 64 * g, w1_codes, w1_plane)
+            deal_w(w2_raw[0], 0, w2_low[g], 0, nc.vector.tensor_copy, 64 * g, 64 * g + 64)
         quantize_w(w1_high, 0, 2, w1_codes, w1_plane, 2)
-        w2_low = [keep.tile([P, 2, 64, PACK], BF16, name="w2_low_%d" % g, tag="w2_low_%d" % g, align_bytes=64) for g in range(2)]
-        for u in range(2):
-            for g in range(2):
-                deal_w(w2_raw[u], 2 * u, w2_low[g], 0, nc.vector.tensor_copy, 64 * g, 64 * g + 64)
+        for g in range(2):
+            deal_w(w2_raw[1], 2, w2_low[g], 0, nc.vector.tensor_copy, 64 * g, 64 * g + 64)
         for g in range(2):
             for t in range(2):
                 quantize_part(w2_low[g], t, 64 * g, w2_codes, w2_plane)
@@ -178,10 +195,9 @@ def tile_picked_edgecv_relu_e_kernel(
         centre = keep.tile([P, PACK, V], F32, tag="w2_low_0", align_bytes=64)
         for t in range(PACK):
             fetch_centre(t)
-        w2_high = [held.tile([P, 2, 64, PACK], BF16, name="w2_high_%d" % g, offset=3072 + 1024 * g, align_bytes=64) for g in range(2)]
+        w2_high = held.tile([P, 2, P, PACK], BF16, name="w2_high", offset=0, align_bytes=64)
         for u in range(2):
-            for g in range(2):
-                deal_w(w2_raw[u], 2 * u, w2_high[g], 2, nc.scalar.copy, 64 * g, 64 * g + 64)
+            deal_high(w2_raw[u], 2 * u, w2_high)
 
         woven = [keep.tile([P, 2, V, 2], BF16, name="woven_%d" % d) for d in range(3)]
         pieces = [(0, 128), (128, 192), (192, 256)]
@@ -194,9 +210,7 @@ def tile_picked_edgecv_relu_e_kernel(
         for d in range(2):
             for t in range(2):
                 fetch_edge(low_edge[d][:, t, :], t, d, 0, V)
-        for g in range(2):
-            for t in range(2):
-                quantize_part(w2_high[g], t, 2 * P + 64 * g, w2_codes, w2_plane)
+        quantize_w(w2_high, 0, 2, w2_codes, w2_plane, 2)
         for t in (2, 3):
             whole_product(e_rows, w2_codes, w2_plane, t, "acc", 6)
         for d in range(2):

@@ -16,6 +16,7 @@ ADD = mybir.AluOpType.add
 MULT = mybir.AluOpType.mult
 MAX = mybir.AluOpType.max
 RELU = mybir.ActivationFunctionType.Relu
+COPY = mybir.ActivationFunctionType.Copy
 
 P = 128
 PACK = 4
@@ -29,6 +30,7 @@ def tile_picked_edgecv_relu_e_kernel(
     nc = tc.nc
     with ExitStack() as ctx:
         keep = ctx.enter_context(tc.tile_pool(name="keep", bufs=1))
+        held = ctx.enter_context(tc.tile_pool(name="held", bufs=1))
         psum = ctx.enter_context(tc.psum_pool(name="psum", bufs=1))
 
         def load_list(source, name):
@@ -36,16 +38,17 @@ def tile_picked_edgecv_relu_e_kernel(
             nc.sync.dma_start(tile[:], source)
             return tile
 
-        def load_w(w, j0, j1, name):
-            raw = keep.tile([P, j1 - j0, H], F32, name="%s_raw_%d" % (name, j0))
-            nc.sync.dma_start(raw[:], w.rearrange("(p j) c -> p j c", j=PACK)[:, j0:j1, :])
-            return raw
-
         def weave(target, source, copy):
             copy(target.rearrange("p (c i) t -> p c t i", i=4), source.rearrange("p t (c i) -> p c t i", i=4))
 
-        def relu(target, source):
+        def scalar_relu(target, source):
             nc.scalar.activation(target, source, RELU)
+
+        def vector_relu(target, source):
+            nc.vector.tensor_scalar_max(target, source, 0.0)
+
+        def scalar_gather(target, source):
+            nc.scalar.activation(target, source, COPY)
 
         def deal_w(raw, j0, dealt, t0, copy, m0=0, m1=P):
             copy(
@@ -57,30 +60,31 @@ def tile_picked_edgecv_relu_e_kernel(
             cols = slice(c0, c0 + values.shape[1] // PACK)
             nc.vector.quantize_mx(out=codes[:, cols].bitcast(FP8X4), scales=plane[:, cols], in_=values)
 
-        def quantize_w(dealt, i0, i1, codes, plane, t0):
-            quantize(codes, plane, t0 * P, dealt[:, i0:i1, :, :].rearrange("p t m j -> p (t m j)"))
-
-        def quantize_part(dealt, t, m0, codes, plane):
-            quantize(codes, plane, t * P + m0, dealt[:, t, :, :].rearrange("p m j -> p (m j)"))
-
         def larger(target, a, b):
             nc.vector.tensor_tensor(target, a, b, MAX)
 
-        x_rows = xT.rearrange("(p u e) c -> p u e c", u=2, e=2)
+        x_rows = xT.rearrange("(p j) c -> p j c", j=PACK)
+        w1_rows = w1.rearrange("(p j) c -> p j c", j=PACK)
+        w2_rows = w2.rearrange("(p j) c -> p j c", j=PACK)
 
-        def load_pair(u, c0, c1):
-            raw = keep.tile([P, 2, c1 - c0], F32, name="x_raw_%d_%d" % (u, c0))
-            nc.sync.dma_start(raw[:], x_rows[:, u, :, c0:c1])
+        def load_plane(j):
+            raw = keep.tile([P, T], F32, name="x_raw_%d" % j)
+            nc.sync.dma_start(raw[:], x_rows[:, j, :])
             return raw
 
-        x_chunks = [(0, 0, 1024), (1, 0, 512), (1, 512, 1024)]
-        x_raw = [load_pair(*x_chunks[0])]
+        def load_w2(u):
+            raw = keep.tile([P, 2, H], F32, name="w2_raw_%d" % u)
+            nc.sync.dma_start(raw[:], w2_rows[:, 2 * u : 2 * u + 2, :])
+            return raw
+
+        x_raw = [load_plane(0)]
         offs_sb = load_list(offs, "offs_sb")
-        x_raw.extend(load_pair(*chunk) for chunk in x_chunks[1:])
-        w1_raw = [load_w(w1, 2 * u, 2 * u + 2, "w1") for u in range(2)]
-        w2_raw = [load_w(w2, 2 * u, 2 * u + 2, "w2") for u in range(2)]
-        cen_sb = load_list(cen, "cen_sb")
+        x_raw.extend(load_plane(j) for j in range(1, PACK))
+        w2_raw = [load_w2(u) for u in range(2)]
         pos_sb = [load_list(pos, "pos_sb_%d" % d) for d, pos in enumerate((pos1, pos2, pos3, pos4))]
+        w1_raw = held.tile([P, PACK, H], F32, name="w1_raw", offset=0, align_bytes=64)
+        nc.sync.dma_start(w1_raw[:], w1_rows)
+        cen_sb = load_list(cen, "cen_sb")
 
         w3_codes = keep.tile([P, N], U32, align_bytes=64)
         nc.sync.dma_start(w3_codes[:].bitcast(I32), w3_words[0].rearrange("p n t -> p (n t)").bitcast(I32))
@@ -89,164 +93,104 @@ def tile_picked_edgecv_relu_e_kernel(
         for q in range(4):
             nc.sync.dma_start(w3_plane[32 * q : 32 * q + 4, :].bitcast(I32), w3_scales[0, 4 * q : 4 * q + 4, :].bitcast(I32))
 
-        x_pairs = [keep.tile([P, T, 2], BF16, name="x_pairs_%d" % u) for u in range(2)]
-        x_picked = [keep.tile([P, HALF_S, 2], U32, name="x_picked_%d" % h, align_bytes=64) for h in range(2)]
+        x_picked = [keep.tile([P, PACK, HALF_S], BF16, name="x_picked_%d" % h) for h in range(2)]
+        for j in range(PACK):
+            for h, gather in enumerate((nc.vector.tensor_copy, scalar_gather)):
+                gather(x_picked[h][:, j, :], x_raw[j][:].indirect(offs_sb[:, h * 16 : (h + 1) * 16]))
+        x_woven = [keep.tile([P, HALF_S, PACK], BF16, name="x_woven_%d" % h, align_bytes=64) for h in range(2)]
         x_codes = keep.tile([P, S], U32, align_bytes=64)
         x_plane = keep.tile([P, S], U8, align_bytes=64)
-
-        def product(acc, codes, plane, t, cols):
-            nc.tensor.matmul_mx(
-                out=acc,
-                lhsT=codes[:, t * P : (t + 1) * P].bitcast(FP8X4),
-                lhsT_scale=plane[:, t * P : (t + 1) * P],
-                rhs=x_codes[:, cols].bitcast(FP8X4),
-                rhs_scale=x_plane[:, cols],
-                start=True,
-                stop=True,
-            )
-
-        def whole_product(rows, codes, plane, t, bank="acc", bufs=3):
-            acc = psum.tile([P, S], F32, name=bank, tag=bank, bufs=bufs)
-            product(acc[:], codes, plane, t, slice(0, S))
-            nc.scalar.copy(rows[t][:], acc[:])
-
-        def quantize_x(h):
-            quantize(x_codes, x_plane, h * HALF_S, x_picked[h][:].rearrange("p c u -> p (c u)").bitcast(BF16))
-
-        def pair_x(index, c0, c1, copy):
-            u, base = x_chunks[index][0:2]
-            weave(x_pairs[u][:, base + c0 : base + c1, :], x_raw[index][:, :, c0:c1], copy)
-
-        x_rows_picked = keep.tile([P, 2, S], U32)
-
-        def pick_x(u, c0, c1):
-            window = x_pairs[u][:].rearrange("p c e -> p (c e)").bitcast(U32)
-            nc.vector.tensor_copy(x_rows_picked[:, u, c0:c1], window.indirect(offs_sb[:, c0 // 16 : c1 // 16]))
-
-        def join_x(h):
-            nc.vector.tensor_copy(x_picked[h][:].bitcast(I32), x_rows_picked[:, :, h * HALF_S : (h + 1) * HALF_S].bitcast(I32).rearrange("p u c -> p c u"))
-
-        pair_x(0, 0, 640, nc.vector.tensor_copy)
-        pair_x(0, 640, 1024, nc.scalar.copy)
-        pick_x(0, 0, S)
-        pair_x(1, 0, 512, nc.scalar.copy)
-        pair_x(2, 0, 352, nc.vector.tensor_copy)
-        pair_x(2, 352, 512, nc.scalar.copy)
-        pick_x(1, 0, HALF_S)
-        pick_x(1, HALF_S, S)
-        join_x(0)
-        join_x(1)
+        weave(x_woven[0][:], x_picked[0][:], nc.vector.tensor_copy)
+        weave(x_woven[1][:, 0:128, :], x_picked[1][:, :, 0:128], nc.scalar.copy)
+        weave(x_woven[1][:, 128:256, :], x_picked[1][:, :, 128:256], nc.vector.tensor_copy)
+        for h in range(2):
+            quantize(x_codes, x_plane, h * HALF_S, x_woven[h][:].rearrange("p c t -> p (c t)"))
 
         w1_codes = keep.tile([P, H], U32, align_bytes=64)
         w1_plane = keep.tile([P, H], U8, align_bytes=64)
         w2_codes = keep.tile([P, H], U32, align_bytes=64)
         w2_plane = keep.tile([P, H], U8, align_bytes=64)
         e_rows = [keep.tile([P, S], F32, name="e_rows_%d" % t) for t in range(PACK)]
-        held = ctx.enter_context(tc.tile_pool(name="held", bufs=1))
         y_rows = [keep.tile([P, S], F32, name="y_rows_%d" % t) for t in range(PACK)]
 
-        def deal_high(raw, j0, dealt):
-            nc.gpsimd.tensor_scalar(
-                dealt[:, :, :, j0 : j0 + 2].rearrange("p t m j -> p m t j"),
-                raw[:].rearrange("p j (m t) -> p m t j", t=PACK)[:, :, 2:4, :],
-                1.0,
-                0.0,
-                MULT,
-                ADD,
+        def product(rows, codes, plane, t, c0, c1, copy):
+            acc = psum.tile([P, c1 - c0], F32, name="acc", tag="acc", bufs=8)
+            nc.tensor.matmul_mx(
+                out=acc[:],
+                lhsT=codes[:, t * P : (t + 1) * P].bitcast(FP8X4),
+                lhsT_scale=plane[:, t * P : (t + 1) * P],
+                rhs=x_codes[:, c0:c1].bitcast(FP8X4),
+                rhs_scale=x_plane[:, c0:c1],
+                start=True,
+                stop=True,
             )
+            copy(rows[t][:, c0:c1], acc[:])
 
-        def fetch_centre(t):
-            nc.vector.tensor_copy(centre[:, t, :], y_rows[t][:].indirect(cen_sb[:]))
-
-        def fetch_edge(target, t, d, v0, v1):
-            nc.vector.tensor_tensor(target, e_rows[t][:].indirect(pos_sb[d][:, v0 // 16 : v1 // 16]), centre[:, t, v0:v1], ADD)
-
-        w1_low = keep.tile([P, 2, P, PACK], BF16, align_bytes=64)
-        w1_high = keep.tile([P, 2, P, PACK], BF16, align_bytes=64)
-        deal_w(w1_raw[0], 0, w1_low, 0, nc.scalar.copy)
-        deal_high(w1_raw[0], 0, w1_high)
-        deal_w(w1_raw[1], 2, w1_low, 0, nc.scalar.copy)
-        deal_w(w1_raw[1], 2, w1_high, 2, nc.scalar.copy)
-        quantize_x(0)
-        quantize_x(1)
-        for t in range(2):
-            quantize_w(w1_low, t, t + 1, w1_codes, w1_plane, t)
-        w2_low = [
-            keep.tile([P, 2, 64, PACK], BF16, name="w2_low_0", tag="w2_low_0", align_bytes=64),
-            held.tile([P, 2, 64, PACK], BF16, name="w2_low_1", offset=0, align_bytes=64),
-        ]
+        w2_low = [keep.tile([P, 2, 64, PACK], BF16, name="w2_low_%d" % g, align_bytes=64) for g in range(2)]
+        w2_high = keep.tile([P, 2, P, PACK], BF16, tag="dealt", align_bytes=64)
         for g in range(2):
-            deal_w(w2_raw[0], 0, w2_low[g], 0, nc.vector.tensor_copy, 64 * g, 64 * g + 64)
-        quantize_w(w1_high, 0, 2, w1_codes, w1_plane, 2)
+            deal_w(w2_raw[0], 0, w2_low[g], 0, nc.scalar.copy, 64 * g, 64 * g + 64)
+        deal_w(w2_raw[0], 0, w2_high, 2, nc.scalar.copy)
         for g in range(2):
             deal_w(w2_raw[1], 2, w2_low[g], 0, nc.vector.tensor_copy, 64 * g, 64 * g + 64)
-        for g in range(2):
-            for t in range(2):
-                quantize_part(w2_low[g], t, 64 * g, w2_codes, w2_plane)
-        for h in range(PACK):
-            cols = slice(h * P, (h + 1) * P)
-            acc_half = psum.tile([P, P], F32, name="acc_half", tag="acc", bufs=6)
-            product(acc_half[:], w1_codes, w1_plane, 0, cols)
-            nc.scalar.copy(y_rows[0][:, cols], acc_half[:])
-        for t in range(1, PACK):
-            whole_product(y_rows, w1_codes, w1_plane, t, "acc", 6)
+        deal_w(w2_raw[1], 2, w2_high, 2, nc.scalar.copy)
         for t in range(2):
-            whole_product(e_rows, w2_codes, w2_plane, t, "acc", 6)
-        centre = keep.tile([P, PACK, V], F32, tag="w2_low_0", align_bytes=64)
+            for g in range(2):
+                quantize(w2_codes, w2_plane, t * P + 64 * g, w2_low[g][:, t, :, :].rearrange("p m j -> p (m j)"))
+        quantize(w2_codes, w2_plane, 2 * P, w2_high[:].rearrange("p t m j -> p (t m j)"))
+
+        product(e_rows, w2_codes, w2_plane, 0, 0, HALF_S, nc.vector.tensor_copy)
+        product(e_rows, w2_codes, w2_plane, 0, HALF_S, S, nc.scalar.copy)
+
+        w1_dealt = keep.tile([P, PACK, P, PACK], BF16, tag="dealt", align_bytes=64)
+        nc.gpsimd.tensor_scalar(
+            w1_dealt[:].rearrange("p t m j -> p m t j"),
+            w1_raw[:].rearrange("p j (m t) -> p m t j", t=PACK),
+            1.0,
+            0.0,
+            MULT,
+            ADD,
+        )
+        quantize(w1_codes, w1_plane, 0, w1_dealt[:].rearrange("p t m j -> p (t m j)"))
+
+        near = [[keep.tile([P, 2, V], F32, name="near_%d_%d" % (t, u)) for u in range(2)] for t in range(PACK)]
+
+        def fetch(t, d, gather):
+            gather(near[t][d // 2][:, d % 2, :], e_rows[t][:].indirect(pos_sb[d][:]))
+
         for t in range(PACK):
-            fetch_centre(t)
-        w2_high = held.tile([P, 2, P, PACK], BF16, name="w2_high", offset=0, align_bytes=64)
-        for u in range(2):
-            deal_high(w2_raw[u], 2 * u, w2_high)
+            if t + 1 < PACK:
+                product(e_rows, w2_codes, w2_plane, t + 1, 0, S, nc.scalar.copy)
+            for d in range(4):
+                fetch(t, d, nc.vector.tensor_copy if d < 2 and t < 3 else scalar_gather)
+        for t in range(PACK):
+            product(y_rows, w1_codes, w1_plane, t, 0, S, nc.scalar.copy)
 
-        woven = [keep.tile([P, 2, V, 2], BF16, name="woven_%d" % d) for d in range(3)]
-        pieces = [(0, 128), (128, 192), (192, 256)]
-        last = [keep.tile([P, 2, v1 - v0, 2], BF16, name="last_%d" % v0) for v0, v1 in pieces]
-        first_max = keep.tile([P, 2, V, 2], BF16)
-        second_max = [keep.tile([P, 2, v1 - v0, 2], BF16, name="second_max_%d" % v0) for v0, v1 in pieces]
-        low_edge = [keep.tile([P, 2, V], F32, name="low_edge_%d" % d) for d in range(2)]
-        high_edge = [keep.tile([P, 2, V], F32, name="high_edge_%d" % d) for d in range(3)]
+        pair_max = [held.tile([P, 2, V], F32, name="pair_max_%d" % t, offset=t * 2 * V * 4, align_bytes=64) for t in range(PACK)]
+        top = [keep.tile([P, V], F32, name="top_%d" % t) for t in range(PACK)]
+        sums = keep.tile([P, PACK, V], F32)
 
-        for d in range(2):
-            for t in range(2):
-                fetch_edge(low_edge[d][:, t, :], t, d, 0, V)
-        quantize_w(w2_high, 0, 2, w2_codes, w2_plane, 2)
-        for t in (2, 3):
-            whole_product(e_rows, w2_codes, w2_plane, t, "acc", 6)
-        for d in range(2):
-            weave(woven[d][:, 0, :, :], low_edge[d][:], relu)
-        late_edge = held.tile([P, 2, 2, V], F32, offset=0, align_bytes=64)
-        for d in (2, 3):
-            for t in range(2):
-                fetch_edge(late_edge[:, d - 2, t, :], t, d, 0, V)
-        weave(woven[2][:, 0, :, :], late_edge[:, 0, :, :], relu)
-        for h, (v0, v1) in enumerate(pieces):
-            weave(last[h][:, 0, :, :], late_edge[:, 1, :, v0:v1], relu)
-        for d in range(3):
-            for t in (2, 3):
-                fetch_edge(high_edge[d][:, t - 2, :], t, d, 0, V)
-            weave(woven[d][:, 1, :, :], high_edge[d][:], relu)
-        last_edge = [keep.tile([P, 2, HALF_V], F32, name="last_edge_%d" % h) for h in range(2)]
+        def add_centre(t, v0, v1):
+            nc.vector.tensor_tensor(sums[:, t, v0:v1], y_rows[t][:].indirect(cen_sb[:, v0 // 16 : v1 // 16]), top[t][:, v0:v1], ADD)
 
-        def fetch_last(h):
-            for t in (2, 3):
-                fetch_edge(last_edge[h][:, t - 2, :], t, 3, h * HALF_V, (h + 1) * HALF_V)
-            for g, (v0, v1) in enumerate(pieces):
-                if v0 // HALF_V == h:
-                    weave(last[g][:, 1, :, :], last_edge[h][:, :, v0 - h * HALF_V : v1 - h * HALF_V], relu)
+        for t0 in (0, 2):
+            for t in (t0, t0 + 1):
+                larger(pair_max[t][:], near[t][0][:], near[t][1][:])
+            for t in (t0, t0 + 1):
+                larger(top[t][:], pair_max[t][:, 0, :], pair_max[t][:, 1, :])
+        for t in range(3):
+            add_centre(t, 0, V)
+        for h in range(2):
+            add_centre(3, h * HALF_V, (h + 1) * HALF_V)
 
-        def project(h):
-            v0, v1 = pieces[h]
-            z_woven = keep.tile([P, v1 - v0, PACK], BF16, name="z_woven_%d" % h, align_bytes=64)
-            larger(
-                z_woven[:].rearrange("p v (g e) -> p v g e", g=2),
-                first_max[:, :, v0:v1, :].rearrange("p g v e -> p v g e"),
-                second_max[h][:].rearrange("p g v e -> p v g e"),
-            )
-            z_codes = keep.tile([P, v1 - v0], U32, name="z_codes_%d" % h, align_bytes=64)
-            z_plane = keep.tile([P, v1 - v0], U8, name="z_plane_%d" % h, align_bytes=64)
-            quantize(z_codes, z_plane, 0, z_woven[:].rearrange("p v t -> p (v t)"))
-            acc_out = psum.tile([P, v1 - v0], F32, name="acc_out", tag="acc", bufs=6)
+        z_woven = [keep.tile([P, HALF_V, PACK], BF16, name="z_woven_%d" % h, align_bytes=64) for h in range(2)]
+        for h, relu in enumerate((scalar_relu, vector_relu)):
+            weave(z_woven[h][:], sums[:, :, h * HALF_V : (h + 1) * HALF_V], relu)
+        for h, copy in enumerate((nc.scalar.copy, nc.vector.tensor_copy)):
+            z_codes = keep.tile([P, HALF_V], U32, name="z_codes_%d" % h, align_bytes=64)
+            z_plane = keep.tile([P, HALF_V], U8, name="z_plane_%d" % h, align_bytes=64)
+            quantize(z_codes, z_plane, 0, z_woven[h][:].rearrange("p v t -> p (v t)"))
+            acc_out = psum.tile([P, HALF_V], F32, name="acc_out", tag="acc", bufs=8)
             nc.tensor.matmul_mx(
                 out=acc_out[:],
                 lhsT=w3_codes[:].bitcast(FP8X4),
@@ -256,15 +200,6 @@ def tile_picked_edgecv_relu_e_kernel(
                 start=True,
                 stop=True,
             )
-            result = keep.tile([P, v1 - v0], F32, name="result_%d" % h)
-            (nc.scalar.copy, nc.scalar.copy, nc.vector.tensor_copy)[h](result[:], acc_out[:])
-            nc.sync.dma_start(out[:, v0:v1], result[:])
-
-        fetch_last(0)
-        fetch_last(1)
-        larger(first_max[:], woven[0][:], woven[1][:])
-        for h, (v0, v1) in enumerate(pieces):
-            larger(second_max[h][:], woven[2][:, :, v0:v1, :], last[h][:])
-        project(0)
-        project(1)
-        project(2)
+            result = keep.tile([P, HALF_V], F32, name="result_%d" % h)
+            copy(result[:], acc_out[:])
+            nc.sync.dma_start(out[:, h * HALF_V : (h + 1) * HALF_V], result[:])

@@ -50,10 +50,10 @@ def tile_picked_edgecv_relu_e_kernel(
         def scalar_gather(target, source):
             nc.scalar.activation(target, source, COPY)
 
-        def deal_w(raw, j0, dealt, t0, copy, m0=0, m1=P):
+        def deal_w(raw, dealt, t0, copy):
             copy(
-                dealt[:, :, :, j0 : j0 + raw.shape[1]].rearrange("p t (c i) j -> p c t i j", i=2),
-                raw[:].rearrange("p j (c i t) -> p c t i j", i=2, t=PACK)[:, m0 // 2 : m1 // 2, t0 : t0 + dealt.shape[1], :, :],
+                dealt.rearrange("p t m j -> p m t j"),
+                raw.rearrange("p j (m t) -> p m t j", t=PACK)[:, :, t0 : t0 + dealt.shape[1], :],
             )
 
         def quantize(codes, plane, c0, values):
@@ -72,15 +72,11 @@ def tile_picked_edgecv_relu_e_kernel(
             nc.sync.dma_start(raw[:], x_rows[:, j, :])
             return raw
 
-        def load_w2(u):
-            raw = keep.tile([P, 2, H], F32, name="w2_raw_%d" % u)
-            nc.sync.dma_start(raw[:], w2_rows[:, 2 * u : 2 * u + 2, :])
-            return raw
-
-        x_raw = [load_plane(0)]
         offs_sb = load_list(offs, "offs_sb")
-        x_raw.extend(load_plane(j) for j in range(1, PACK))
-        w2_raw = [load_w2(u) for u in range(2)]
+        x_raw = [load_plane(j) for j in range(PACK)]
+        w2_raw = [keep.tile([P, PACK, H // 2], F32, name="w2_raw_%d" % g) for g in range(2)]
+        for g in range(2):
+            nc.sync.dma_start(w2_raw[g][:], w2_rows[:, :, g * H // 2 : (g + 1) * H // 2])
         pos_sb = [load_list(pos, "pos_sb_%d" % d) for d, pos in enumerate((pos1, pos2, pos3, pos4))]
         w1_raw = held.tile([P, PACK, H], F32, name="w1_raw", offset=0, align_bytes=64)
         nc.sync.dma_start(w1_raw[:], w1_rows)
@@ -93,18 +89,23 @@ def tile_picked_edgecv_relu_e_kernel(
         for q in range(4):
             nc.sync.dma_start(w3_plane[32 * q : 32 * q + 4, :].bitcast(I32), w3_scales[0, 4 * q : 4 * q + 4, :].bitcast(I32))
 
-        x_picked = [keep.tile([P, PACK, HALF_S], BF16, name="x_picked_%d" % h) for h in range(2)]
+        warm_in = keep.tile([P, 1], F32)
+        warm_out = keep.tile([P, 1], F32)
+        nc.vector.memset(warm_in[:], 0.0)
+        nc.scalar.activation(warm_out[:], warm_in[:], RELU)
+        SPLIT = 320
+        x_picked = [keep.tile([P, 2, S - SPLIT], BF16, name="x_picked_%d" % u) for u in range(2)]
+        x_woven = keep.tile([P, S, PACK], BF16, align_bytes=64)
         for j in range(PACK):
-            for h, gather in enumerate((nc.vector.tensor_copy, scalar_gather)):
-                gather(x_picked[h][:, j, :], x_raw[j][:].indirect(offs_sb[:, h * 16 : (h + 1) * 16]))
-        x_woven = [keep.tile([P, HALF_S, PACK], BF16, name="x_woven_%d" % h, align_bytes=64) for h in range(2)]
-        x_codes = keep.tile([P, S], U32, align_bytes=64)
+            nc.vector.tensor_copy(x_woven[:, 0:SPLIT, j], x_raw[j][:].indirect(offs_sb[:, 0 : SPLIT // 16]))
+            scalar_gather(x_picked[j // 2][:, j % 2, :], x_raw[j][:].indirect(offs_sb[:, SPLIT // 16 : S // 16]))
+            if j % 2 == 1:
+                weave(x_woven[:, SPLIT:S, j - 1 : j + 1], x_picked[j // 2][:], nc.scalar.copy)
         x_plane = keep.tile([P, S], U8, align_bytes=64)
-        weave(x_woven[0][:], x_picked[0][:], nc.vector.tensor_copy)
-        weave(x_woven[1][:, 0:128, :], x_picked[1][:, :, 0:128], nc.scalar.copy)
-        weave(x_woven[1][:, 128:256, :], x_picked[1][:, :, 128:256], nc.vector.tensor_copy)
-        for h in range(2):
-            quantize(x_codes, x_plane, h * HALF_S, x_woven[h][:].rearrange("p c t -> p (c t)"))
+
+        def quantize_x(h):
+            quantize(x_codes, x_plane, h * HALF_S, x_woven[:, h * HALF_S : (h + 1) * HALF_S, :].rearrange("p c t -> p (c t)"))
+
 
         w1_codes = keep.tile([P, H], U32, align_bytes=64)
         w1_plane = keep.tile([P, H], U8, align_bytes=64)
@@ -112,6 +113,10 @@ def tile_picked_edgecv_relu_e_kernel(
         w2_plane = keep.tile([P, H], U8, align_bytes=64)
         e_rows = [keep.tile([P, S], F32, name="e_rows_%d" % t) for t in range(PACK)]
         y_rows = [keep.tile([P, S], F32, name="y_rows_%d" % t) for t in range(PACK)]
+
+        DEALT = PACK * H * 4
+        FIRST = DEALT + 4096
+        x_codes = held.tile([P, S], U32, name="x_codes", offset=FIRST, align_bytes=64)
 
         def product(rows, codes, plane, t, c0, c1, copy):
             acc = psum.tile([P, c1 - c0], F32, name="acc", tag="acc", bufs=8)
@@ -126,71 +131,105 @@ def tile_picked_edgecv_relu_e_kernel(
             )
             copy(rows[t][:, c0:c1], acc[:])
 
-        w2_low = [keep.tile([P, 2, 64, PACK], BF16, name="w2_low_%d" % g, align_bytes=64) for g in range(2)]
-        w2_high = keep.tile([P, 2, P, PACK], BF16, tag="dealt", align_bytes=64)
-        for g in range(2):
-            deal_w(w2_raw[0], 0, w2_low[g], 0, nc.scalar.copy, 64 * g, 64 * g + 64)
-        deal_w(w2_raw[0], 0, w2_high, 2, nc.scalar.copy)
-        for g in range(2):
-            deal_w(w2_raw[1], 2, w2_low[g], 0, nc.vector.tensor_copy, 64 * g, 64 * g + 64)
-        deal_w(w2_raw[1], 2, w2_high, 2, nc.scalar.copy)
+        def gpsimd_deal(dealt, raw, t0):
+            nc.gpsimd.tensor_scalar(
+                dealt[:].rearrange("p t m j -> p m t j"),
+                raw[:].rearrange("p j (m t) -> p m t j", t=PACK)[:, :, t0 : t0 + dealt.shape[1], :],
+                1.0,
+                0.0,
+                MULT,
+                ADD,
+            )
+
+        w2_first = [held.tile([P, 1, 64, PACK], BF16, name="w2_first_%d" % t, offset=FIRST + 2048 * t, align_bytes=64) for t in range(2)]
+        w2_second = keep.tile([P, 2, 64, PACK], BF16, align_bytes=64)
+        w2_high = held.tile([P, 2, P, PACK], BF16, name="w2_high", offset=DEALT, align_bytes=64)
         for t in range(2):
-            for g in range(2):
-                quantize(w2_codes, w2_plane, t * P + 64 * g, w2_low[g][:, t, :, :].rearrange("p m j -> p (m j)"))
-        quantize(w2_codes, w2_plane, 2 * P, w2_high[:].rearrange("p t m j -> p (t m j)"))
+            deal_w(w2_raw[0][:], w2_first[t][:], t, nc.vector.tensor_copy)
+        for t in range(2):
+            quantize(w2_codes, w2_plane, t * 64, w2_first[t][:].rearrange("p t m j -> p (t m j)"))
+        quantize_x(0)
+        quantize_x(1)
+        deal_w(w2_raw[1][:], w2_second[:], 0, nc.vector.tensor_copy)
+        for g in range(2):
+            deal_w(w2_raw[g][:], w2_high[:, :, 64 * g : 64 * g + 64, :], 2, nc.scalar.copy)
+        quantize(w2_codes, w2_plane, P, w2_second[:].rearrange("p t m j -> p (t m j)"))
 
         product(e_rows, w2_codes, w2_plane, 0, 0, HALF_S, nc.vector.tensor_copy)
         product(e_rows, w2_codes, w2_plane, 0, HALF_S, S, nc.scalar.copy)
 
-        w1_dealt = keep.tile([P, PACK, P, PACK], BF16, tag="dealt", align_bytes=64)
-        nc.gpsimd.tensor_scalar(
-            w1_dealt[:].rearrange("p t m j -> p m t j"),
-            w1_raw[:].rearrange("p j (m t) -> p m t j", t=PACK),
-            1.0,
-            0.0,
-            MULT,
-            ADD,
-        )
+        quantize(w2_codes, w2_plane, 2 * P, w2_high[:].rearrange("p t m j -> p (t m j)"))
+        w1_dealt = held.tile([P, PACK, P, PACK], BF16, name="w1_dealt", offset=DEALT, align_bytes=64)
+        gpsimd_deal(w1_dealt, w1_raw, 0)
         quantize(w1_codes, w1_plane, 0, w1_dealt[:].rearrange("p t m j -> p (t m j)"))
 
-        near = [[keep.tile([P, 2, V], F32, name="near_%d_%d" % (t, u)) for u in range(2)] for t in range(PACK)]
+        near = [[keep.tile([P, 2, V], F32, name="near_%d_%d" % (t, u)) for u in range(2)] for t in range(3)]
+        near.append([held.tile([P, 2, V], F32, name="near_3_%d" % u, offset=DEALT + 2048 * u, align_bytes=64) for u in range(2)])
 
         def fetch(t, d, gather):
             gather(near[t][d // 2][:, d % 2, :], e_rows[t][:].indirect(pos_sb[d][:]))
 
-        for t in range(PACK):
-            if t + 1 < PACK:
-                product(e_rows, w2_codes, w2_plane, t + 1, 0, S, nc.scalar.copy)
+        for t in range(3):
+            product(e_rows, w2_codes, w2_plane, t + 1, 0, S, nc.scalar.copy)
             for d in range(4):
-                fetch(t, d, nc.vector.tensor_copy if d < 2 and t < 3 else scalar_gather)
-        for t in range(PACK):
+                fetch(t, d, nc.vector.tensor_copy if d < 3 - t else scalar_gather)
+        product(y_rows, w1_codes, w1_plane, 2, 0, S, nc.scalar.copy)
+        for d in range(1, 4):
+            fetch(3, d, scalar_gather)
+        for t in (0, 1, 3):
             product(y_rows, w1_codes, w1_plane, t, 0, S, nc.scalar.copy)
 
         pair_max = [held.tile([P, 2, V], F32, name="pair_max_%d" % t, offset=t * 2 * V * 4, align_bytes=64) for t in range(PACK)]
-        top = [keep.tile([P, V], F32, name="top_%d" % t) for t in range(PACK)]
+        TOPS = FIRST + 4096
+        top = [held.tile([P, V], F32, name="top_%d" % t, offset=TOPS + 1024 * (t % 3), align_bytes=64) for t in range(PACK)]
         sums = keep.tile([P, PACK, V], F32)
 
         def add_centre(t, v0, v1):
             nc.vector.tensor_tensor(sums[:, t, v0:v1], y_rows[t][:].indirect(cen_sb[:, v0 // 16 : v1 // 16]), top[t][:, v0:v1], ADD)
 
-        for t0 in (0, 2):
-            for t in (t0, t0 + 1):
-                larger(pair_max[t][:], near[t][0][:], near[t][1][:])
-            for t in (t0, t0 + 1):
-                larger(top[t][:], pair_max[t][:, 0, :], pair_max[t][:, 1, :])
-        for t in range(3):
-            add_centre(t, 0, V)
-        for h in range(2):
-            add_centre(3, h * HALF_V, (h + 1) * HALF_V)
+        def first_max(t):
+            larger(pair_max[t][:], near[t][0][:], near[t][1][:])
 
-        z_woven = [keep.tile([P, HALF_V, PACK], BF16, name="z_woven_%d" % h, align_bytes=64) for h in range(2)]
-        for h, relu in enumerate((scalar_relu, vector_relu)):
-            weave(z_woven[h][:], sums[:, :, h * HALF_V : (h + 1) * HALF_V], relu)
-        for h, copy in enumerate((nc.scalar.copy, nc.vector.tensor_copy)):
-            z_codes = keep.tile([P, HALF_V], U32, name="z_codes_%d" % h, align_bytes=64)
-            z_plane = keep.tile([P, HALF_V], U8, name="z_plane_%d" % h, align_bytes=64)
-            quantize(z_codes, z_plane, 0, z_woven[h][:].rearrange("p v t -> p (v t)"))
-            acc_out = psum.tile([P, HALF_V], F32, name="acc_out", tag="acc", bufs=8)
+        def second_max(target, t):
+            larger(target[:], pair_max[t][:, 0, :], pair_max[t][:, 1, :])
+
+        crossed = [keep.tile([P, V], F32, name="crossed_%d" % g) for g in range(2)]
+        first_max(0)
+        first_max(1)
+        for g in range(2):
+            second_max(crossed[g], g)
+            for t in range(2):
+                nc.sync.dma_start(top[t][64 * g : 64 * g + 64, :], crossed[g][64 * t : 64 * t + 64, :])
+        first_max(2)
+        fetch(3, 0, nc.vector.tensor_copy)
+        second_max(top[2], 2)
+        larger(pair_max[3][:, 0, :], near[3][0][:, 0, :], near[3][1][:, 0, :])
+        add_centre(2, 0, V)
+        late_max = held.tile([P, V], F32, name="late_max", offset=2 * 2 * V * 4, align_bytes=64)
+        larger(late_max[:], near[3][0][:, 1, :], near[3][1][:, 1, :])
+        add_centre(0, 0, V)
+        add_centre(1, 0, V)
+        pieces = [(0, HALF_V), (HALF_V, V)]
+        for v0, v1 in pieces:
+            larger(top[3][:, v0:v1], pair_max[3][:, 0, v0:v1], late_max[:, v0:v1])
+        centre = keep.tile([P, V], F32)
+        scalar_gather(centre[:], y_rows[3][:].indirect(cen_sb[:]))
+        pieces = [(0, 128), (128, 192), (192, 256)]
+        for v0, v1 in pieces:
+            nc.vector.tensor_tensor(sums[:, 3, v0:v1], centre[:, v0:v1], top[3][:, v0:v1], ADD)
+
+        z_woven = [keep.tile([P, v1 - v0, PACK], BF16, name="z_woven_%d" % v0, align_bytes=64) for v0, v1 in pieces]
+        for t0 in (0, 2):
+            weave(z_woven[0][:, :, t0 : t0 + 2], sums[:, t0 : t0 + 2, 0:HALF_V], scalar_relu)
+        for g in (1, 2):
+            weave(z_woven[g][:], sums[:, :, pieces[g][0] : pieces[g][1]], vector_relu)
+        result = [keep.tile([P, HALF_V], F32, name="result_%d" % h) for h in range(2)]
+        for g, copy in enumerate((nc.scalar.copy, nc.scalar.copy, nc.vector.tensor_copy)):
+            v0, v1 = pieces[g]
+            z_codes = keep.tile([P, v1 - v0], U32, name="z_codes_%d" % v0, align_bytes=64)
+            z_plane = keep.tile([P, v1 - v0], U8, name="z_plane_%d" % v0, align_bytes=64)
+            quantize(z_codes, z_plane, 0, z_woven[g][:].rearrange("p v t -> p (v t)"))
+            acc_out = psum.tile([P, v1 - v0], F32, name="acc_out", tag="acc", bufs=8)
             nc.tensor.matmul_mx(
                 out=acc_out[:],
                 lhsT=w3_codes[:].bitcast(FP8X4),
@@ -200,6 +239,7 @@ def tile_picked_edgecv_relu_e_kernel(
                 start=True,
                 stop=True,
             )
-            result = keep.tile([P, HALF_V], F32, name="result_%d" % h)
-            copy(result[:], acc_out[:])
-            nc.sync.dma_start(out[:, h * HALF_V : (h + 1) * HALF_V], result[:])
+            h = v0 // HALF_V
+            copy(result[h][:, v0 - h * HALF_V : v1 - h * HALF_V], acc_out[:])
+            if v1 % HALF_V == 0:
+                nc.sync.dma_start(out[:, v1 - HALF_V : v1], result[h][:])

@@ -20,8 +20,12 @@ COPY = mybir.ActivationFunctionType.Copy
 
 P = 128
 PACK = 4
+HALF_P = P // 2
 HALF_S = S // 2
 HALF_V = V // 2
+HALF_H = H // 2
+VECTOR_POINTS = 320
+KIB = 1024
 
 
 def tile_picked_edgecv_relu_e_kernel(
@@ -38,6 +42,9 @@ def tile_picked_edgecv_relu_e_kernel(
             nc.sync.dma_start(tile[:], source)
             return tile
 
+        def entries(list_tile, first, last):
+            return list_tile[:, first // 16 : last // 16]
+
         def weave(target, source, copy):
             copy(target.rearrange("p (c i) t -> p c t i", i=4), source.rearrange("p t (c i) -> p c t i", i=4))
 
@@ -50,7 +57,10 @@ def tile_picked_edgecv_relu_e_kernel(
         def scalar_gather(target, source):
             nc.scalar.activation(target, source, COPY)
 
-        def deal_w(raw, dealt, t0, copy):
+        def gpsimd_copy(target, source):
+            nc.gpsimd.tensor_scalar(target, source, 1.0, 0.0, MULT, ADD)
+
+        def deal(raw, dealt, t0, copy):
             copy(
                 dealt.rearrange("p t m j -> p m t j"),
                 raw.rearrange("p j (m t) -> p m t j", t=PACK)[:, :, t0 : t0 + dealt.shape[1], :],
@@ -68,17 +78,18 @@ def tile_picked_edgecv_relu_e_kernel(
         w2_rows = w2.rearrange("(p j) c -> p j c", j=PACK)
 
         def load_plane(j):
-            raw = keep.tile([P, T], F32, name="x_raw_%d" % j)
+            raw = keep.tile([P, T], F32, name="x_raw_%d" % j, align_bytes=256)
             nc.sync.dma_start(raw[:], x_rows[:, j, :])
             return raw
 
+        x_raw = [load_plane(0)]
         offs_sb = load_list(offs, "offs_sb")
-        x_raw = [load_plane(j) for j in range(PACK)]
-        w2_raw = [keep.tile([P, PACK, H // 2], F32, name="w2_raw_%d" % g) for g in range(2)]
+        x_raw.extend(load_plane(j) for j in range(1, PACK))
+        w2_raw = [keep.tile([P, PACK, HALF_H], F32, name="w2_raw_%d" % g, align_bytes=256) for g in range(2)]
         for g in range(2):
-            nc.sync.dma_start(w2_raw[g][:], w2_rows[:, :, g * H // 2 : (g + 1) * H // 2])
+            nc.sync.dma_start(w2_raw[g][:], w2_rows[:, :, g * HALF_H : (g + 1) * HALF_H])
         pos_sb = [load_list(pos, "pos_sb_%d" % d) for d, pos in enumerate((pos1, pos2, pos3, pos4))]
-        w1_raw = held.tile([P, PACK, H], F32, name="w1_raw", offset=0, align_bytes=64)
+        w1_raw = held.tile([P, PACK, H], F32, name="w1_raw", offset=0, align_bytes=256)
         nc.sync.dma_start(w1_raw[:], w1_rows)
         cen_sb = load_list(cen, "cen_sb")
 
@@ -93,30 +104,25 @@ def tile_picked_edgecv_relu_e_kernel(
         warm_out = keep.tile([P, 1], F32)
         nc.vector.memset(warm_in[:], 0.0)
         nc.scalar.activation(warm_out[:], warm_in[:], RELU)
-        SPLIT = 320
-        x_picked = [keep.tile([P, 2, S - SPLIT], BF16, name="x_picked_%d" % u) for u in range(2)]
+
+        x_picked = [keep.tile([P, 2, S - VECTOR_POINTS], BF16, name="x_picked_%d" % u) for u in range(2)]
         x_woven = keep.tile([P, S, PACK], BF16, align_bytes=64)
         for j in range(PACK):
-            nc.vector.tensor_copy(x_woven[:, 0:SPLIT, j], x_raw[j][:].indirect(offs_sb[:, 0 : SPLIT // 16]))
-            scalar_gather(x_picked[j // 2][:, j % 2, :], x_raw[j][:].indirect(offs_sb[:, SPLIT // 16 : S // 16]))
+            nc.vector.tensor_copy(x_woven[:, 0:VECTOR_POINTS, j], x_raw[j][:].indirect(entries(offs_sb, 0, VECTOR_POINTS)))
+            scalar_gather(x_picked[j // 2][:, j % 2, :], x_raw[j][:].indirect(entries(offs_sb, VECTOR_POINTS, S)))
             if j % 2 == 1:
-                weave(x_woven[:, SPLIT:S, j - 1 : j + 1], x_picked[j // 2][:], nc.scalar.copy)
+                weave(x_woven[:, VECTOR_POINTS:S, j - 1 : j + 1], x_picked[j // 2][:], nc.scalar.copy)
+        DEALT = 8 * KIB
+        FIRST = 12 * KIB
+        NEAR = 16 * KIB
+        x_codes = held.tile([P, S], U32, name="x_codes", offset=FIRST, align_bytes=64)
         x_plane = keep.tile([P, S], U8, align_bytes=64)
-
-        def quantize_x(h):
-            quantize(x_codes, x_plane, h * HALF_S, x_woven[:, h * HALF_S : (h + 1) * HALF_S, :].rearrange("p c t -> p (c t)"))
-
 
         w1_codes = keep.tile([P, H], U32, align_bytes=64)
         w1_plane = keep.tile([P, H], U8, align_bytes=64)
         w2_codes = keep.tile([P, H], U32, align_bytes=64)
         w2_plane = keep.tile([P, H], U8, align_bytes=64)
         e_rows = [keep.tile([P, S], F32, name="e_rows_%d" % t) for t in range(PACK)]
-        y_rows = [keep.tile([P, S], F32, name="y_rows_%d" % t) for t in range(PACK)]
-
-        DEALT = PACK * H * 4
-        FIRST = DEALT + 4096
-        x_codes = held.tile([P, S], U32, name="x_codes", offset=FIRST, align_bytes=64)
 
         def product(rows, codes, plane, t, c0, c1, copy):
             acc = psum.tile([P, c1 - c0], F32, name="acc", tag="acc", bufs=8)
@@ -131,104 +137,89 @@ def tile_picked_edgecv_relu_e_kernel(
             )
             copy(rows[t][:, c0:c1], acc[:])
 
-        def gpsimd_deal(dealt, raw, t0):
-            nc.gpsimd.tensor_scalar(
-                dealt[:].rearrange("p t m j -> p m t j"),
-                raw[:].rearrange("p j (m t) -> p m t j", t=PACK)[:, :, t0 : t0 + dealt.shape[1], :],
-                1.0,
-                0.0,
-                MULT,
-                ADD,
-            )
+        def flat(dealt):
+            return dealt.rearrange("p t m j -> p (t m j)")
 
-        w2_first = [held.tile([P, 1, 64, PACK], BF16, name="w2_first_%d" % t, offset=FIRST + 2048 * t, align_bytes=64) for t in range(2)]
-        w2_second = keep.tile([P, 2, 64, PACK], BF16, align_bytes=64)
-        w2_high = held.tile([P, 2, P, PACK], BF16, name="w2_high", offset=DEALT, align_bytes=64)
+        low_first = [held.tile([P, 1, HALF_P, PACK], BF16, name="low_first_%d" % t, offset=FIRST + 2 * KIB * t, align_bytes=64) for t in range(2)]
+        low_second = keep.tile([P, 2, HALF_P, PACK], BF16, align_bytes=64)
+        high = held.tile([P, 2, P, PACK], BF16, name="high", offset=DEALT, align_bytes=64)
         for t in range(2):
-            deal_w(w2_raw[0][:], w2_first[t][:], t, nc.vector.tensor_copy)
+            deal(w2_raw[0][:], low_first[t][:], t, nc.vector.tensor_copy)
         for t in range(2):
-            quantize(w2_codes, w2_plane, t * 64, w2_first[t][:].rearrange("p t m j -> p (t m j)"))
-        quantize_x(0)
-        quantize_x(1)
-        deal_w(w2_raw[1][:], w2_second[:], 0, nc.vector.tensor_copy)
+            quantize(w2_codes, w2_plane, t * HALF_P, flat(low_first[t][:]))
+        for c0 in (0, HALF_S):
+            quantize(x_codes, x_plane, c0, x_woven[:, c0 : c0 + HALF_S, :].rearrange("p c t -> p (c t)"))
+        deal(w2_raw[1][:], low_second[:], 0, nc.vector.tensor_copy)
         for g in range(2):
-            deal_w(w2_raw[g][:], w2_high[:, :, 64 * g : 64 * g + 64, :], 2, nc.scalar.copy)
-        quantize(w2_codes, w2_plane, P, w2_second[:].rearrange("p t m j -> p (t m j)"))
-
+            deal(w2_raw[g][:], high[:, :, g * HALF_P : (g + 1) * HALF_P], 2, nc.scalar.copy)
+        quantize(w2_codes, w2_plane, P, flat(low_second[:]))
         product(e_rows, w2_codes, w2_plane, 0, 0, HALF_S, nc.vector.tensor_copy)
         product(e_rows, w2_codes, w2_plane, 0, HALF_S, S, nc.scalar.copy)
-
-        quantize(w2_codes, w2_plane, 2 * P, w2_high[:].rearrange("p t m j -> p (t m j)"))
+        quantize(w2_codes, w2_plane, 2 * P, flat(high[:]))
         w1_dealt = held.tile([P, PACK, P, PACK], BF16, name="w1_dealt", offset=DEALT, align_bytes=64)
-        gpsimd_deal(w1_dealt, w1_raw, 0)
-        quantize(w1_codes, w1_plane, 0, w1_dealt[:].rearrange("p t m j -> p (t m j)"))
+        deal(w1_raw[:], w1_dealt[:], 0, gpsimd_copy)
 
-        near = [[keep.tile([P, 2, V], F32, name="near_%d_%d" % (t, u)) for u in range(2)] for t in range(3)]
-        near.append([held.tile([P, 2, V], F32, name="near_3_%d" % u, offset=DEALT + 2048 * u, align_bytes=64) for u in range(2)])
+        def fetch(target, t, d, v0, v1, gather):
+            gather(target[:, v0:v1], e_rows[t][:].indirect(entries(pos_sb[d], v0, v1)))
 
-        def fetch(t, d, gather):
-            gather(near[t][d // 2][:, d % 2, :], e_rows[t][:].indirect(pos_sb[d][:]))
-
+        near_01 = [held.tile([P, 2, 2, V], F32, name="near_01_%d" % u, offset=NEAR + 4 * KIB * u, align_bytes=64) for u in range(2)]
+        near_2 = held.tile([P, 2, 2, V], F32, name="near_2", offset=NEAR + 8 * KIB, align_bytes=64)
         for t in range(3):
             product(e_rows, w2_codes, w2_plane, t + 1, 0, S, nc.scalar.copy)
             for d in range(4):
-                fetch(t, d, nc.vector.tensor_copy if d < 3 - t else scalar_gather)
-        product(y_rows, w1_codes, w1_plane, 2, 0, S, nc.scalar.copy)
-        for d in range(1, 4):
-            fetch(3, d, scalar_gather)
-        for t in (0, 1, 3):
-            product(y_rows, w1_codes, w1_plane, t, 0, S, nc.scalar.copy)
+                target = near_01[d // 2][:, t, d % 2, :] if t < 2 else near_2[:, d // 2, d % 2, :]
+                fetch(target, t, d, 0, V, nc.vector.tensor_copy if d < 3 - t else scalar_gather)
 
-        pair_max = [held.tile([P, 2, V], F32, name="pair_max_%d" % t, offset=t * 2 * V * 4, align_bytes=64) for t in range(PACK)]
-        TOPS = FIRST + 4096
-        top = [held.tile([P, V], F32, name="top_%d" % t, offset=TOPS + 1024 * (t % 3), align_bytes=64) for t in range(PACK)]
+        pair_01 = held.tile([P, 2, 2, V], F32, name="pair_01", offset=0, align_bytes=64)
+        larger(pair_01[:], near_01[0][:], near_01[1][:])
+        quantize(w1_codes, w1_plane, 0, flat(w1_dealt[:]))
+        crossed = keep.tile([P, 2, V], F32)
+        larger(crossed[:], pair_01[:, :, 0, :], pair_01[:, :, 1, :])
+        top = [keep.tile([P, V], F32, name="top_%d" % t) for t in range(PACK)]
+        for g in range(2):
+            for t in range(2):
+                nc.sync.dma_start(top[t][HALF_P * g : HALF_P * (g + 1), :], crossed[HALF_P * t : HALF_P * (t + 1), g, :])
+
+        near_3_free = held.tile([P, 2, V], F32, name="near_3_free", offset=4 * KIB, align_bytes=64)
+        for d in (2, 3):
+            fetch(near_3_free[:, d - 2, :], 3, d, 0, V, scalar_gather)
+        near_3_held = held.tile([P, 2, V], F32, name="near_3_held", offset=0, align_bytes=64)
+        fetch(near_3_held[:, 1, :], 3, 1, 0, V, scalar_gather)
+        pair_2 = held.tile([P, 2, V], F32, name="pair_2", offset=NEAR, align_bytes=64)
+        larger(pair_2[:], near_2[:, 0], near_2[:, 1])
+        fetch(near_3_held[:, 0, :], 3, 0, 0, V, nc.vector.tensor_copy)
+        y_places = (4 * KIB, 6 * KIB, NEAR + 8 * KIB, NEAR)
+        y_rows = [held.tile([P, S], F32, name="y_rows_%d" % t, offset=y_places[t], align_bytes=64) for t in range(PACK)]
+        product(y_rows, w1_codes, w1_plane, 2, 0, S, nc.scalar.copy)
+
         sums = keep.tile([P, PACK, V], F32)
 
         def add_centre(t, v0, v1):
-            nc.vector.tensor_tensor(sums[:, t, v0:v1], y_rows[t][:].indirect(cen_sb[:, v0 // 16 : v1 // 16]), top[t][:, v0:v1], ADD)
+            nc.vector.tensor_tensor(sums[:, t, v0:v1], y_rows[t][:].indirect(entries(cen_sb, v0, v1)), top[t][:, v0:v1], ADD)
 
-        def first_max(t):
-            larger(pair_max[t][:], near[t][0][:], near[t][1][:])
-
-        def second_max(target, t):
-            larger(target[:], pair_max[t][:, 0, :], pair_max[t][:, 1, :])
-
-        crossed = [keep.tile([P, V], F32, name="crossed_%d" % g) for g in range(2)]
-        first_max(0)
-        first_max(1)
-        for g in range(2):
-            second_max(crossed[g], g)
-            for t in range(2):
-                nc.sync.dma_start(top[t][64 * g : 64 * g + 64, :], crossed[g][64 * t : 64 * t + 64, :])
-        first_max(2)
-        fetch(3, 0, nc.vector.tensor_copy)
-        second_max(top[2], 2)
-        larger(pair_max[3][:, 0, :], near[3][0][:, 0, :], near[3][1][:, 0, :])
-        add_centre(2, 0, V)
-        late_max = held.tile([P, V], F32, name="late_max", offset=2 * 2 * V * 4, align_bytes=64)
-        larger(late_max[:], near[3][0][:, 1, :], near[3][1][:, 1, :])
+        larger(top[2][:], pair_2[:, 0, :], pair_2[:, 1, :])
+        product(y_rows, w1_codes, w1_plane, 3, 0, S, nc.scalar.copy)
+        pair_3 = held.tile([P, 2, V], F32, name="pair_3", offset=6 * KIB, align_bytes=64)
+        larger(pair_3[:], near_3_held[:], near_3_free[:])
+        product(y_rows, w1_codes, w1_plane, 0, 0, S, nc.scalar.copy)
+        add_centre(2, 0, HALF_V)
+        larger(top[3][:], pair_3[:, 0, :], pair_3[:, 1, :])
+        product(y_rows, w1_codes, w1_plane, 1, 0, S, nc.scalar.copy)
+        add_centre(2, HALF_V, V)
+        add_centre(3, 0, V)
+        pieces = ((0, 128), (128, 192), (192, 256))
+        z_woven = keep.tile([P, V, PACK], BF16, align_bytes=64)
+        weave(z_woven[:, :, 2:4], sums[:, 2:4, :], scalar_relu)
         add_centre(0, 0, V)
-        add_centre(1, 0, V)
-        pieces = [(0, HALF_V), (HALF_V, V)]
         for v0, v1 in pieces:
-            larger(top[3][:, v0:v1], pair_max[3][:, 0, v0:v1], late_max[:, v0:v1])
-        centre = keep.tile([P, V], F32)
-        scalar_gather(centre[:], y_rows[3][:].indirect(cen_sb[:]))
-        pieces = [(0, 128), (128, 192), (192, 256)]
-        for v0, v1 in pieces:
-            nc.vector.tensor_tensor(sums[:, 3, v0:v1], centre[:, v0:v1], top[3][:, v0:v1], ADD)
-
-        z_woven = [keep.tile([P, v1 - v0, PACK], BF16, name="z_woven_%d" % v0, align_bytes=64) for v0, v1 in pieces]
-        for t0 in (0, 2):
-            weave(z_woven[0][:, :, t0 : t0 + 2], sums[:, t0 : t0 + 2, 0:HALF_V], scalar_relu)
-        for g in (1, 2):
-            weave(z_woven[g][:], sums[:, :, pieces[g][0] : pieces[g][1]], vector_relu)
+            add_centre(1, v0, v1)
+        for (v0, v1), relu in zip(pieces, (scalar_relu, vector_relu, scalar_relu)):
+            weave(z_woven[:, v0:v1, 0:2], sums[:, 0:2, v0:v1], relu)
         result = [keep.tile([P, HALF_V], F32, name="result_%d" % h) for h in range(2)]
-        for g, copy in enumerate((nc.scalar.copy, nc.scalar.copy, nc.vector.tensor_copy)):
-            v0, v1 = pieces[g]
+        for (v0, v1), copy in zip(pieces, (nc.scalar.copy, nc.scalar.copy, nc.vector.tensor_copy)):
             z_codes = keep.tile([P, v1 - v0], U32, name="z_codes_%d" % v0, align_bytes=64)
             z_plane = keep.tile([P, v1 - v0], U8, name="z_plane_%d" % v0, align_bytes=64)
-            quantize(z_codes, z_plane, 0, z_woven[g][:].rearrange("p v t -> p (v t)"))
+            quantize(z_codes, z_plane, 0, z_woven[:, v0:v1, :].rearrange("p v t -> p (v t)"))
             acc_out = psum.tile([P, v1 - v0], F32, name="acc_out", tag="acc", bufs=8)
             nc.tensor.matmul_mx(
                 out=acc_out[:],

@@ -168,7 +168,11 @@ def tile_picked_edgecv_relu_e_kernel(
             product(e_rows, w2_codes, w2_plane, t + 1, 0, S, nc.scalar.copy)
             for d in range(4):
                 target = near_01[d // 2][:, t, d % 2, :] if t < 2 else near_2[:, d // 2, d % 2, :]
-                fetch(target, t, d, 0, V, nc.vector.tensor_copy if d < 3 - t else scalar_gather)
+                if (t, d) == (2, 1):
+                    fetch(target, t, d, 0, HALF_V, nc.vector.tensor_copy)
+                    fetch(target, t, d, HALF_V, V, scalar_gather)
+                else:
+                    fetch(target, t, d, 0, V, nc.vector.tensor_copy if d < 3 - t else scalar_gather)
 
         pair_01 = held.tile([P, 2, 2, V], F32, name="pair_01", offset=0, align_bytes=64)
         larger(pair_01[:], near_01[0][:], near_01[1][:])

@@ -174,9 +174,13 @@ def tile_picked_edgecv_relu_e_kernel(
                 else:
                     fetch(target, t, d, 0, V, nc.vector.tensor_copy if d < 3 - t else scalar_gather)
 
+        near_3 = [held.tile([P, 2, V], F32, name="near_3_%d" % u, offset=NEAR + (12 + 2 * u) * KIB, align_bytes=64) for u in range(2)]
+        for d in range(4):
+            fetch(near_3[d // 2][:, d % 2, :], 3, d, 0, V, nc.vector.tensor_copy if d == 0 else scalar_gather)
+
         pair_01 = held.tile([P, 2, 2, V], F32, name="pair_01", offset=0, align_bytes=64)
         larger(pair_01[:], near_01[0][:], near_01[1][:])
-        quantize(w1_codes, w1_plane, 0, flat(w1_dealt[:]))
+        quantize(w1_codes, w1_plane, 2 * P, flat(w1_dealt[:, 2:4]))
         crossed = keep.tile([P, 2, V], F32)
         larger(crossed[:], pair_01[:, :, 0, :], pair_01[:, :, 1, :])
         top = [keep.tile([P, V], F32, name="top_%d" % t) for t in range(PACK)]
@@ -184,15 +188,10 @@ def tile_picked_edgecv_relu_e_kernel(
             for t in range(2):
                 nc.sync.dma_start(top[t][HALF_P * g : HALF_P * (g + 1), :], crossed[HALF_P * t : HALF_P * (t + 1), g, :])
 
-        near_3_free = held.tile([P, 2, V], F32, name="near_3_free", offset=4 * KIB, align_bytes=64)
-        for d in (2, 3):
-            fetch(near_3_free[:, d - 2, :], 3, d, 0, V, scalar_gather)
-        near_3_held = held.tile([P, 2, V], F32, name="near_3_held", offset=0, align_bytes=64)
-        fetch(near_3_held[:, 1, :], 3, 1, 0, V, scalar_gather)
         pair_2 = held.tile([P, 2, V], F32, name="pair_2", offset=NEAR, align_bytes=64)
         larger(pair_2[:], near_2[:, 0], near_2[:, 1])
-        fetch(near_3_held[:, 0, :], 3, 0, 0, V, nc.vector.tensor_copy)
-        y_places = (4 * KIB, 6 * KIB, NEAR + 8 * KIB, NEAR)
+        quantize(w1_codes, w1_plane, 0, flat(w1_dealt[:, 0:2]))
+        y_places = (NEAR + 12 * KIB, 0, NEAR + 8 * KIB, NEAR)
         y_rows = [held.tile([P, S], F32, name="y_rows_%d" % t, offset=y_places[t], align_bytes=64) for t in range(PACK)]
         product(y_rows, w1_codes, w1_plane, 2, 0, S, nc.scalar.copy)
 
@@ -203,8 +202,8 @@ def tile_picked_edgecv_relu_e_kernel(
 
         larger(top[2][:], pair_2[:, 0, :], pair_2[:, 1, :])
         product(y_rows, w1_codes, w1_plane, 3, 0, S, nc.scalar.copy)
-        pair_3 = held.tile([P, 2, V], F32, name="pair_3", offset=6 * KIB, align_bytes=64)
-        larger(pair_3[:], near_3_held[:], near_3_free[:])
+        pair_3 = held.tile([P, 2, V], F32, name="pair_3", offset=0, align_bytes=64)
+        larger(pair_3[:], near_3[0][:], near_3[1][:])
         product(y_rows, w1_codes, w1_plane, 0, 0, S, nc.scalar.copy)
         add_centre(2, 0, HALF_V)
         larger(top[3][:], pair_3[:, 0, :], pair_3[:, 1, :])

@@ -180,19 +180,17 @@ def tile_picked_edgecv_relu_e_kernel(
 
         pair_01 = held.tile([P, 2, 2, V], F32, name="pair_01", offset=0, align_bytes=64)
         larger(pair_01[:], near_01[0][:], near_01[1][:])
-        quantize(w1_codes, w1_plane, 2 * P, flat(w1_dealt[:, 2:4]))
+        quantize(w1_codes, w1_plane, 0, flat(w1_dealt[:]))
         crossed = keep.tile([P, 2, V], F32)
         larger(crossed[:], pair_01[:, :, 0, :], pair_01[:, :, 1, :])
         top = [keep.tile([P, V], F32, name="top_%d" % t) for t in range(PACK)]
-        for g in range(2):
-            for t in range(2):
+        for t in range(2):
+            for g in range(2):
                 nc.sync.dma_start(top[t][HALF_P * g : HALF_P * (g + 1), :], crossed[HALF_P * t : HALF_P * (t + 1), g, :])
 
         pair_2 = held.tile([P, 2, V], F32, name="pair_2", offset=NEAR, align_bytes=64)
         larger(pair_2[:], near_2[:, 0], near_2[:, 1])
-        quantize(w1_codes, w1_plane, 0, flat(w1_dealt[:, 0:2]))
-        y_places = (NEAR + 12 * KIB, 0, NEAR + 8 * KIB, NEAR)
-        y_rows = [held.tile([P, S], F32, name="y_rows_%d" % t, offset=y_places[t], align_bytes=64) for t in range(PACK)]
+        y_rows = [keep.tile([P, S], F32, name="y_rows_%d" % t) for t in range(PACK)]
         product(y_rows, w1_codes, w1_plane, 2, 0, S, nc.scalar.copy)
 
         sums = keep.tile([P, PACK, V], F32)
@@ -200,16 +198,14 @@ def tile_picked_edgecv_relu_e_kernel(
         def add_centre(t, v0, v1):
             nc.vector.tensor_tensor(sums[:, t, v0:v1], y_rows[t][:].indirect(entries(cen_sb, v0, v1)), top[t][:, v0:v1], ADD)
 
-        larger(top[2][:], pair_2[:, 0, :], pair_2[:, 1, :])
-        product(y_rows, w1_codes, w1_plane, 3, 0, S, nc.scalar.copy)
         pair_3 = held.tile([P, 2, V], F32, name="pair_3", offset=0, align_bytes=64)
         larger(pair_3[:], near_3[0][:], near_3[1][:])
-        product(y_rows, w1_codes, w1_plane, 0, 0, S, nc.scalar.copy)
-        add_centre(2, 0, HALF_V)
-        larger(top[3][:], pair_3[:, 0, :], pair_3[:, 1, :])
-        product(y_rows, w1_codes, w1_plane, 1, 0, S, nc.scalar.copy)
-        add_centre(2, HALF_V, V)
-        add_centre(3, 0, V)
+        for t, pair in ((2, pair_2), (3, pair_3)):
+            larger(top[t][:], pair[:, 0, :], pair[:, 1, :])
+        for t in (3, 0, 1):
+            product(y_rows, w1_codes, w1_plane, t, 0, S, nc.scalar.copy)
+        for t in (2, 3):
+            add_centre(t, 0, V)
         pieces = ((0, 128), (128, 192), (192, 256))
         z_woven = keep.tile([P, V, PACK], BF16, align_bytes=64)
         weave(z_woven[:, :, 2:4], sums[:, 2:4, :], scalar_relu)

@@ -25,6 +25,7 @@ HALF_S = S // 2
 HALF_V = V // 2
 HALF_H = H // 2
 VECTOR_POINTS = 320
+SHARED = 96
 KIB = 1024
 
 
@@ -163,20 +164,17 @@ def tile_picked_edgecv_relu_e_kernel(
             gather(target[:, v0:v1], e_rows[t][:].indirect(entries(pos_sb[d], v0, v1)))
 
         near_01 = [held.tile([P, 2, 2, V], F32, name="near_01_%d" % u, offset=NEAR + 4 * KIB * u, align_bytes=64) for u in range(2)]
-        near_2 = held.tile([P, 2, 2, V], F32, name="near_2", offset=NEAR + 8 * KIB, align_bytes=64)
-        for t in range(3):
-            product(e_rows, w2_codes, w2_plane, t + 1, 0, S, nc.scalar.copy)
-            for d in range(4):
-                target = near_01[d // 2][:, t, d % 2, :] if t < 2 else near_2[:, d // 2, d % 2, :]
+        near_23 = [keep.tile([P, 2, 2, V], F32, name="near_23_%d" % u) for u in range(2)]
+        for t, vector_lists in enumerate((3, 2, 1, 1)):
+            if t + 1 < PACK:
+                product(e_rows, w2_codes, w2_plane, t + 1, 0, S, nc.scalar.copy)
+            for d in (0, 2, 1, 3) if t == 3 else range(4):
+                target = (near_01 if t < 2 else near_23)[d // 2][:, t % 2, d % 2, :]
                 if (t, d) == (2, 1):
-                    fetch(target, t, d, 0, HALF_V, nc.vector.tensor_copy)
-                    fetch(target, t, d, HALF_V, V, scalar_gather)
+                    fetch(target, t, d, 0, SHARED, nc.vector.tensor_copy)
+                    fetch(target, t, d, SHARED, V, scalar_gather)
                 else:
-                    fetch(target, t, d, 0, V, nc.vector.tensor_copy if d < 3 - t else scalar_gather)
-
-        near_3 = [held.tile([P, 2, V], F32, name="near_3_%d" % u, offset=NEAR + (12 + 2 * u) * KIB, align_bytes=64) for u in range(2)]
-        for d in range(4):
-            fetch(near_3[d // 2][:, d % 2, :], 3, d, 0, V, nc.vector.tensor_copy if d == 0 else scalar_gather)
+                    fetch(target, t, d, 0, V, nc.vector.tensor_copy if d < vector_lists else scalar_gather)
 
         pair_01 = held.tile([P, 2, 2, V], F32, name="pair_01", offset=0, align_bytes=64)
         larger(pair_01[:], near_01[0][:], near_01[1][:])
@@ -188,8 +186,10 @@ def tile_picked_edgecv_relu_e_kernel(
             for g in range(2):
                 nc.sync.dma_start(top[t][HALF_P * g : HALF_P * (g + 1), :], crossed[HALF_P * t : HALF_P * (t + 1), g, :])
 
-        pair_2 = held.tile([P, 2, V], F32, name="pair_2", offset=NEAR, align_bytes=64)
-        larger(pair_2[:], near_2[:, 0], near_2[:, 1])
+        pair_23 = held.tile([P, 4, V], F32, name="pair_23", offset=NEAR, align_bytes=64)
+        slots = [near[:].rearrange("p t d v -> p (t d) v") for near in near_23]
+        for s0, s1 in ((0, 3), (3, 4)):
+            larger(pair_23[:, s0:s1], slots[0][:, s0:s1], slots[1][:, s0:s1])
         y_rows = [keep.tile([P, S], F32, name="y_rows_%d" % t) for t in range(PACK)]
         product(y_rows, w1_codes, w1_plane, 2, 0, S, nc.scalar.copy)
 
@@ -198,10 +198,8 @@ def tile_picked_edgecv_relu_e_kernel(
         def add_centre(t, v0, v1):
             nc.vector.tensor_tensor(sums[:, t, v0:v1], y_rows[t][:].indirect(entries(cen_sb, v0, v1)), top[t][:, v0:v1], ADD)
 
-        pair_3 = held.tile([P, 2, V], F32, name="pair_3", offset=0, align_bytes=64)
-        larger(pair_3[:], near_3[0][:], near_3[1][:])
-        for t, pair in ((2, pair_2), (3, pair_3)):
-            larger(top[t][:], pair[:, 0, :], pair[:, 1, :])
+        for u in range(2):
+            larger(top[2 + u][:], pair_23[:, 2 * u, :], pair_23[:, 2 * u + 1, :])
         for t in (3, 0, 1):
             product(y_rows, w1_codes, w1_plane, t, 0, S, nc.scalar.copy)
         for t in (2, 3):

@@ -24,8 +24,7 @@ HALF_P = P // 2
 HALF_S = S // 2
 HALF_V = V // 2
 HALF_H = H // 2
-VECTOR_POINTS = 320
-SHARED = 96
+VECTOR_POINTS = 256
 KIB = 1024
 
 
@@ -89,9 +88,12 @@ def tile_picked_edgecv_relu_e_kernel(
         w2_raw = [keep.tile([P, PACK, HALF_H], F32, name="w2_raw_%d" % g, align_bytes=256) for g in range(2)]
         for g in range(2):
             nc.sync.dma_start(w2_raw[g][:], w2_rows[:, :, g * HALF_H : (g + 1) * HALF_H])
-        pos_sb = [load_list(pos, "pos_sb_%d" % d) for d, pos in enumerate((pos1, pos2, pos3, pos4))]
-        w1_raw = held.tile([P, PACK, H], F32, name="w1_raw", offset=0, align_bytes=256)
-        nc.sync.dma_start(w1_raw[:], w1_rows)
+        pos_last = load_list(pos4, "pos_sb_3")
+        pos_sb = [load_list(pos, "pos_sb_%d" % d) for d, pos in enumerate((pos1, pos2, pos3))] + [pos_last]
+        w1_early = keep.tile([P, 2, H], F32, name="w1_early", align_bytes=256)
+        w1_late = held.tile([P, 2, H], F32, name="w1_late", offset=0, align_bytes=256)
+        nc.sync.dma_start(w1_early[:], w1_rows[:, 0:2, :])
+        nc.sync.dma_start(w1_late[:], w1_rows[:, 2:4, :])
         cen_sb = load_list(cen, "cen_sb")
 
         w3_codes = keep.tile([P, N], U32, align_bytes=64)
@@ -106,26 +108,24 @@ def tile_picked_edgecv_relu_e_kernel(
         nc.vector.memset(warm_in[:], 0.0)
         nc.scalar.activation(warm_out[:], warm_in[:], RELU)
 
-        x_picked = [keep.tile([P, 2, S - VECTOR_POINTS], BF16, name="x_picked_%d" % u) for u in range(2)]
         x_woven = keep.tile([P, S, PACK], BF16, align_bytes=64)
         for j in range(PACK):
             nc.vector.tensor_copy(x_woven[:, 0:VECTOR_POINTS, j], x_raw[j][:].indirect(entries(offs_sb, 0, VECTOR_POINTS)))
-            scalar_gather(x_picked[j // 2][:, j % 2, :], x_raw[j][:].indirect(entries(offs_sb, VECTOR_POINTS, S)))
-            if j % 2 == 1:
-                weave(x_woven[:, VECTOR_POINTS:S, j - 1 : j + 1], x_picked[j // 2][:], nc.scalar.copy)
+            scalar_gather(x_woven[:, VECTOR_POINTS:S, j], x_raw[j][:].indirect(entries(offs_sb, VECTOR_POINTS, S)))
         DEALT = 8 * KIB
-        FIRST = 12 * KIB
         NEAR = 16 * KIB
-        x_codes = held.tile([P, S], U32, name="x_codes", offset=FIRST, align_bytes=64)
+        x_codes = keep.tile([P, S], U32, align_bytes=64)
         x_plane = keep.tile([P, S], U8, align_bytes=64)
 
         w1_codes = keep.tile([P, H], U32, align_bytes=64)
         w1_plane = keep.tile([P, H], U8, align_bytes=64)
-        w2_codes = keep.tile([P, H], U32, align_bytes=64)
-        w2_plane = keep.tile([P, H], U8, align_bytes=64)
+        low_codes = keep.tile([P, HALF_H], U32, align_bytes=64)
+        low_plane = keep.tile([P, HALF_H], U8, align_bytes=64)
+        high_codes = held.tile([P, HALF_H], U32, name="high_codes", offset=NEAR + 6 * KIB, align_bytes=64)
+        high_plane = keep.tile([P, HALF_H], U8, align_bytes=64)
         e_rows = [keep.tile([P, S], F32, name="e_rows_%d" % t) for t in range(PACK)]
 
-        def product(rows, codes, plane, t, c0, c1, copy):
+        def product(row, codes, plane, t, c0, c1, copy):
             acc = psum.tile([P, c1 - c0], F32, name="acc", tag="acc", bufs=8)
             nc.tensor.matmul_mx(
                 out=acc[:],
@@ -136,48 +136,57 @@ def tile_picked_edgecv_relu_e_kernel(
                 start=True,
                 stop=True,
             )
-            copy(rows[t][:, c0:c1], acc[:])
+            copy(row[:, c0:c1], acc[:])
 
         def flat(dealt):
             return dealt.rearrange("p t m j -> p (t m j)")
 
-        low_first = [held.tile([P, 1, HALF_P, PACK], BF16, name="low_first_%d" % t, offset=FIRST + 2 * KIB * t, align_bytes=64) for t in range(2)]
-        low_second = keep.tile([P, 2, HALF_P, PACK], BF16, align_bytes=64)
-        high = held.tile([P, 2, P, PACK], BF16, name="high", offset=DEALT, align_bytes=64)
-        for t in range(2):
-            deal(w2_raw[0][:], low_first[t][:], t, nc.vector.tensor_copy)
-        for t in range(2):
-            quantize(w2_codes, w2_plane, t * HALF_P, flat(low_first[t][:]))
-        for c0 in (0, HALF_S):
-            quantize(x_codes, x_plane, c0, x_woven[:, c0 : c0 + HALF_S, :].rearrange("p c t -> p (c t)"))
-        deal(w2_raw[1][:], low_second[:], 0, nc.vector.tensor_copy)
-        for g in range(2):
-            deal(w2_raw[g][:], high[:, :, g * HALF_P : (g + 1) * HALF_P], 2, nc.scalar.copy)
-        quantize(w2_codes, w2_plane, P, flat(low_second[:]))
-        product(e_rows, w2_codes, w2_plane, 0, 0, HALF_S, nc.vector.tensor_copy)
-        product(e_rows, w2_codes, w2_plane, 0, HALF_S, S, nc.scalar.copy)
-        quantize(w2_codes, w2_plane, 2 * P, flat(high[:]))
+        low = [keep.tile([P, 2, HALF_P, PACK], BF16, name="low_%d" % g, align_bytes=64) for g in range(2)]
+        high = [held.tile([P, 2, HALF_P, PACK], BF16, name="high_%d" % g, offset=DEALT + g * KIB, align_bytes=64) for g in range(2)]
+
+        def quantize_high(g):
+            for u in range(2):
+                quantize(high_codes, high_plane, u * P + g * HALF_P, flat(high[g][:, u : u + 1]))
+
+        quantize(x_codes, x_plane, 0, x_woven[:].rearrange("p c t -> p (c t)"))
+        deal(w2_raw[0][:], low[0][:], 0, nc.vector.tensor_copy)
+        deal(w2_raw[0][:], high[0][:], 2, nc.scalar.copy)
+        quantize(low_codes, low_plane, 0, flat(low[0][:]))
+        quantize_high(0)
+        deal(w2_raw[1][:], low[1][:], 0, nc.vector.tensor_copy)
+        deal(w2_raw[1][:], high[1][:], 2, nc.vector.tensor_copy)
+        quantize(low_codes, low_plane, P, flat(low[1][:]))
+        product(e_rows[0], low_codes, low_plane, 0, 0, HALF_S, nc.scalar.copy)
+        product(e_rows[0], low_codes, low_plane, 0, HALF_S, S, nc.scalar.copy)
+        quantize_high(1)
         w1_dealt = held.tile([P, PACK, P, PACK], BF16, name="w1_dealt", offset=DEALT, align_bytes=64)
-        deal(w1_raw[:], w1_dealt[:], 0, gpsimd_copy)
+        deal(w1_early[:], w1_dealt[:, :, :, 0:2], 0, gpsimd_copy)
+        deal(w1_late[:], w1_dealt[:, :, :, 2:4], 0, gpsimd_copy)
 
         def fetch(target, t, d, v0, v1, gather):
             gather(target[:, v0:v1], e_rows[t][:].indirect(entries(pos_sb[d], v0, v1)))
 
-        near_01 = [held.tile([P, 2, 2, V], F32, name="near_01_%d" % u, offset=NEAR + 4 * KIB * u, align_bytes=64) for u in range(2)]
+        near_01 = held.tile([P, 2, 2, V], F32, name="near_01", offset=NEAR, align_bytes=64)
+        far_01 = [held.tile([P, 2, V], F32, name="far_01_%d" % t, offset=NEAR + (4 + 2 * t) * KIB, align_bytes=64) for t in range(2)]
         near_23 = [keep.tile([P, 2, 2, V], F32, name="near_23_%d" % u) for u in range(2)]
-        for t, vector_lists in enumerate((3, 2, 1, 1)):
-            if t + 1 < PACK:
-                product(e_rows, w2_codes, w2_plane, t + 1, 0, S, nc.scalar.copy)
+        fetch(far_01[0][:, 1, :], 0, 3, 0, V, scalar_gather)
+        product(e_rows[1], low_codes, low_plane, 1, 0, S, nc.scalar.copy)
+        for t in range(2):
+            product(e_rows[2 + t], high_codes, high_plane, t, 0, S, nc.scalar.copy)
+        for d in range(2):
+            fetch(near_01[:, 0, d, :], 0, d, 0, V, nc.vector.tensor_copy)
+        fetch(far_01[0][:, 0, :], 0, 2, 0, V, nc.vector.tensor_copy)
+        for d in range(2):
+            fetch(near_01[:, 1, d, :], 1, d, 0, V, nc.vector.tensor_copy)
+        for d in range(2):
+            fetch(far_01[1][:, d, :], 1, 2 + d, 0, V, scalar_gather)
+        for t in (2, 3):
             for d in (0, 2, 1, 3) if t == 3 else range(4):
-                target = (near_01 if t < 2 else near_23)[d // 2][:, t % 2, d % 2, :]
-                if (t, d) == (2, 1):
-                    fetch(target, t, d, 0, SHARED, nc.vector.tensor_copy)
-                    fetch(target, t, d, SHARED, V, scalar_gather)
-                else:
-                    fetch(target, t, d, 0, V, nc.vector.tensor_copy if d < vector_lists else scalar_gather)
+                fetch(near_23[d // 2][:, t % 2, d % 2, :], t, d, 0, V, nc.vector.tensor_copy if d == 0 else scalar_gather)
 
         pair_01 = held.tile([P, 2, 2, V], F32, name="pair_01", offset=0, align_bytes=64)
-        larger(pair_01[:], near_01[0][:], near_01[1][:])
+        for t in range(2):
+            larger(pair_01[:, t], near_01[:, t], far_01[t][:])
         quantize(w1_codes, w1_plane, 0, flat(w1_dealt[:]))
         crossed = keep.tile([P, 2, V], F32)
         larger(crossed[:], pair_01[:, :, 0, :], pair_01[:, :, 1, :])
@@ -191,7 +200,7 @@ def tile_picked_edgecv_relu_e_kernel(
         for s0, s1 in ((0, 3), (3, 4)):
             larger(pair_23[:, s0:s1], slots[0][:, s0:s1], slots[1][:, s0:s1])
         y_rows = [keep.tile([P, S], F32, name="y_rows_%d" % t) for t in range(PACK)]
-        product(y_rows, w1_codes, w1_plane, 2, 0, S, nc.scalar.copy)
+        product(y_rows[2], w1_codes, w1_plane, 2, 0, S, nc.scalar.copy)
 
         sums = keep.tile([P, PACK, V], F32)
 
@@ -201,7 +210,7 @@ def tile_picked_edgecv_relu_e_kernel(
         for u in range(2):
             larger(top[2 + u][:], pair_23[:, 2 * u, :], pair_23[:, 2 * u + 1, :])
         for t in (3, 0, 1):
-            product(y_rows, w1_codes, w1_plane, t, 0, S, nc.scalar.copy)
+            product(y_rows[t], w1_codes, w1_plane, t, 0, S, nc.scalar.copy)
         for t in (2, 3):
             add_centre(t, 0, V)
         pieces = ((0, 128), (128, 192), (192, 256))

@@ -25,6 +25,7 @@ HALF_S = S // 2
 HALF_V = V // 2
 HALF_H = H // 2
 VECTOR_POINTS = 256
+SHARED = 96
 KIB = 1024
 
 
@@ -90,10 +91,8 @@ def tile_picked_edgecv_relu_e_kernel(
             nc.sync.dma_start(w2_raw[g][:], w2_rows[:, :, g * HALF_H : (g + 1) * HALF_H])
         pos_last = load_list(pos4, "pos_sb_3")
         pos_sb = [load_list(pos, "pos_sb_%d" % d) for d, pos in enumerate((pos1, pos2, pos3))] + [pos_last]
-        w1_early = keep.tile([P, 2, H], F32, name="w1_early", align_bytes=256)
-        w1_late = held.tile([P, 2, H], F32, name="w1_late", offset=0, align_bytes=256)
-        nc.sync.dma_start(w1_early[:], w1_rows[:, 0:2, :])
-        nc.sync.dma_start(w1_late[:], w1_rows[:, 2:4, :])
+        w1_raw = held.tile([P, PACK, H], F32, name="w1_raw", offset=0, align_bytes=256)
+        nc.sync.dma_start(w1_raw[:], w1_rows)
         cen_sb = load_list(cen, "cen_sb")
 
         w3_codes = keep.tile([P, N], U32, align_bytes=64)
@@ -160,8 +159,7 @@ def tile_picked_edgecv_relu_e_kernel(
         product(e_rows[0], low_codes, low_plane, 0, HALF_S, S, nc.scalar.copy)
         quantize_high(1)
         w1_dealt = held.tile([P, PACK, P, PACK], BF16, name="w1_dealt", offset=DEALT, align_bytes=64)
-        deal(w1_early[:], w1_dealt[:, :, :, 0:2], 0, gpsimd_copy)
-        deal(w1_late[:], w1_dealt[:, :, :, 2:4], 0, gpsimd_copy)
+        deal(w1_raw[:], w1_dealt[:], 0, gpsimd_copy)
 
         def fetch(target, t, d, v0, v1, gather):
             gather(target[:, v0:v1], e_rows[t][:].indirect(entries(pos_sb[d], v0, v1)))
@@ -182,7 +180,12 @@ def tile_picked_edgecv_relu_e_kernel(
             fetch(far_01[1][:, d, :], 1, 2 + d, 0, V, scalar_gather)
         for t in (2, 3):
             for d in (0, 2, 1, 3) if t == 3 else range(4):
-                fetch(near_23[d // 2][:, t % 2, d % 2, :], t, d, 0, V, nc.vector.tensor_copy if d == 0 else scalar_gather)
+                target = near_23[d // 2][:, t % 2, d % 2, :]
+                if (t, d) == (2, 1):
+                    fetch(target, t, d, 0, SHARED, nc.vector.tensor_copy)
+                    fetch(target, t, d, SHARED, V, scalar_gather)
+                else:
+                    fetch(target, t, d, 0, V, nc.vector.tensor_copy if d == 0 else scalar_gather)
 
         pair_01 = held.tile([P, 2, 2, V], F32, name="pair_01", offset=0, align_bytes=64)
         for t in range(2):

@@ -63,8 +63,8 @@ def tile_picked_edgecv_relu_e_kernel(
 
         def deal(raw, dealt, t0, copy):
             copy(
-                dealt.rearrange("p t m j -> p m t j"),
-                raw.rearrange("p j (m t) -> p m t j", t=PACK)[:, :, t0 : t0 + dealt.shape[1], :],
+                dealt.rearrange("p t m j -> p m j t"),
+                raw.rearrange("p j (m t) -> p m j t", t=PACK)[:, :, :, t0 : t0 + dealt.shape[1]],
             )
 
         def quantize(codes, plane, c0, values):
@@ -159,7 +159,7 @@ def tile_picked_edgecv_relu_e_kernel(
         product(e_rows[0], low_codes, low_plane, 0, HALF_S, S, nc.scalar.copy)
         quantize_high(1)
         w1_dealt = held.tile([P, PACK, P, PACK], BF16, name="w1_dealt", offset=DEALT, align_bytes=64)
-        deal(w1_raw[:], w1_dealt[:], 0, gpsimd_copy)
+        gpsimd_copy(w1_dealt[:].rearrange("p t m j -> p m t j"), w1_raw[:].rearrange("p j (m t) -> p m t j", t=PACK))
 
         def fetch(target, t, d, v0, v1, gather):
             gather(target[:, v0:v1], e_rows[t][:].indirect(entries(pos_sb[d], v0, v1)))

@@ -25,7 +25,6 @@ HALF_S = S // 2
 HALF_V = V // 2
 HALF_H = H // 2
 VECTOR_POINTS = 256
-SHARED = 96
 KIB = 1024
 
 
@@ -180,23 +179,18 @@ def tile_picked_edgecv_relu_e_kernel(
             fetch(far_01[1][:, d, :], 1, 2 + d, 0, V, scalar_gather)
         for t in (2, 3):
             for d in (0, 2, 1, 3) if t == 3 else range(4):
-                target = near_23[d // 2][:, t % 2, d % 2, :]
-                if (t, d) == (2, 1):
-                    fetch(target, t, d, 0, SHARED, nc.vector.tensor_copy)
-                    fetch(target, t, d, SHARED, V, scalar_gather)
-                else:
-                    fetch(target, t, d, 0, V, nc.vector.tensor_copy if d == 0 else scalar_gather)
+                fetch(near_23[d // 2][:, t % 2, d % 2, :], t, d, 0, V, nc.vector.tensor_copy if d < 4 - t else scalar_gather)
 
-        pair_01 = held.tile([P, 2, 2, V], F32, name="pair_01", offset=0, align_bytes=64)
-        for t in range(2):
-            larger(pair_01[:, t], near_01[:, t], far_01[t][:])
         quantize(w1_codes, w1_plane, 0, flat(w1_dealt[:]))
-        crossed = keep.tile([P, 2, V], F32)
-        larger(crossed[:], pair_01[:, :, 0, :], pair_01[:, :, 1, :])
+        pair_01 = [held.tile([P, 2, V], F32, name="pair_01_%d" % g, offset=g * DEALT, align_bytes=64) for g in range(2)]
+        for g in range(2):
+            larger(pair_01[g][:], near_01[:, g], far_01[g][:])
         top = [keep.tile([P, V], F32, name="top_%d" % t) for t in range(PACK)]
-        for t in range(2):
-            for g in range(2):
-                nc.sync.dma_start(top[t][HALF_P * g : HALF_P * (g + 1), :], crossed[HALF_P * t : HALF_P * (t + 1), g, :])
+        for g in range(2):
+            crossed = keep.tile([P, V], F32, name="crossed_%d" % g)
+            larger(crossed[:], pair_01[g][:, 0, :], pair_01[g][:, 1, :])
+            for t in range(2):
+                nc.sync.dma_start(top[t][HALF_P * g : HALF_P * (g + 1), :], crossed[HALF_P * t : HALF_P * (t + 1), :])
 
         pair_23 = held.tile([P, 4, V], F32, name="pair_23", offset=NEAR, align_bytes=64)
         slots = [near[:].rearrange("p t d v -> p (t d) v") for near in near_23]
@@ -212,10 +206,13 @@ def tile_picked_edgecv_relu_e_kernel(
 
         for u in range(2):
             larger(top[2 + u][:], pair_23[:, 2 * u, :], pair_23[:, 2 * u + 1, :])
-        for t in (3, 0, 1):
+        product(y_rows[3], w1_codes, w1_plane, 3, 0, S, nc.scalar.copy)
+        centre_2 = keep.tile([P, V], F32)
+        scalar_gather(centre_2[:], y_rows[2][:].indirect(cen_sb[:]))
+        for t in (0, 1):
             product(y_rows[t], w1_codes, w1_plane, t, 0, S, nc.scalar.copy)
-        for t in (2, 3):
-            add_centre(t, 0, V)
+        add_centre(3, 0, V)
+        nc.vector.tensor_tensor(sums[:, 2, :], centre_2[:], top[2][:], ADD)
         pieces = ((0, 128), (128, 192), (192, 256))
         z_woven = keep.tile([P, V, PACK], BF16, align_bytes=64)
         weave(z_woven[:, :, 2:4], sums[:, 2:4, :], scalar_relu)

@@ -25,6 +25,7 @@ HALF_S = S // 2
 HALF_V = V // 2
 HALF_H = H // 2
 VECTOR_POINTS = 256
+SHARED = 128
 KIB = 1024
 
 
@@ -179,7 +180,12 @@ def tile_picked_edgecv_relu_e_kernel(
             fetch(far_01[1][:, d, :], 1, 2 + d, 0, V, scalar_gather)
         for t in (2, 3):
             for d in (0, 2, 1, 3) if t == 3 else range(4):
-                fetch(near_23[d // 2][:, t % 2, d % 2, :], t, d, 0, V, nc.vector.tensor_copy if d < 4 - t else scalar_gather)
+                target = near_23[d // 2][:, t % 2, d % 2, :]
+                if (t, d) == (2, 1):
+                    fetch(target, t, d, 0, SHARED, nc.vector.tensor_copy)
+                    fetch(target, t, d, SHARED, V, scalar_gather)
+                else:
+                    fetch(target, t, d, 0, V, nc.vector.tensor_copy if d == 0 else scalar_gather)
 
         quantize(w1_codes, w1_plane, 0, flat(w1_dealt[:]))
         pair_01 = [held.tile([P, 2, V], F32, name="pair_01_%d" % g, offset=g * DEALT, align_bytes=64) for g in range(2)]

@@ -25,7 +25,6 @@ HALF_S = S // 2
 HALF_V = V // 2
 HALF_H = H // 2
 VECTOR_POINTS = 256
-SHARED = 128
 KIB = 1024
 
 
@@ -180,12 +179,7 @@ def tile_picked_edgecv_relu_e_kernel(
             fetch(far_01[1][:, d, :], 1, 2 + d, 0, V, scalar_gather)
         for t in (2, 3):
             for d in (0, 2, 1, 3) if t == 3 else range(4):
-                target = near_23[d // 2][:, t % 2, d % 2, :]
-                if (t, d) == (2, 1):
-                    fetch(target, t, d, 0, SHARED, nc.vector.tensor_copy)
-                    fetch(target, t, d, SHARED, V, scalar_gather)
-                else:
-                    fetch(target, t, d, 0, V, nc.vector.tensor_copy if d == 0 else scalar_gather)
+                fetch(near_23[d // 2][:, t % 2, d % 2, :], t, d, 0, V, nc.vector.tensor_copy if d == 0 else scalar_gather)
 
         quantize(w1_codes, w1_plane, 0, flat(w1_dealt[:]))
         pair_01 = [held.tile([P, 2, V], F32, name="pair_01_%d" % g, offset=g * DEALT, align_bytes=64) for g in range(2)]
@@ -212,21 +206,20 @@ def tile_picked_edgecv_relu_e_kernel(
 
         for u in range(2):
             larger(top[2 + u][:], pair_23[:, 2 * u, :], pair_23[:, 2 * u + 1, :])
-        product(y_rows[3], w1_codes, w1_plane, 3, 0, S, nc.scalar.copy)
-        centre_2 = keep.tile([P, V], F32)
-        scalar_gather(centre_2[:], y_rows[2][:].indirect(cen_sb[:]))
-        for t in (0, 1):
+        for t in (3, 1, 0):
             product(y_rows[t], w1_codes, w1_plane, t, 0, S, nc.scalar.copy)
-        add_centre(3, 0, V)
-        nc.vector.tensor_tensor(sums[:, 2, :], centre_2[:], top[2][:], ADD)
+        centre_1 = keep.tile([P, V], F32)
+        scalar_gather(centre_1[:], y_rows[1][:].indirect(cen_sb[:]))
+        for t in (2, 3, 0):
+            add_centre(t, 0, V)
         pieces = ((0, 128), (128, 192), (192, 256))
         z_woven = keep.tile([P, V, PACK], BF16, align_bytes=64)
-        weave(z_woven[:, :, 2:4], sums[:, 2:4, :], scalar_relu)
-        add_centre(0, 0, V)
+        weave(z_woven[:, 0:HALF_V, 2:4], sums[:, 2:4, 0:HALF_V], scalar_relu)
         for v0, v1 in pieces:
-            add_centre(1, v0, v1)
-        for (v0, v1), relu in zip(pieces, (scalar_relu, vector_relu, scalar_relu)):
-            weave(z_woven[:, v0:v1, 0:2], sums[:, 0:2, v0:v1], relu)
+            nc.vector.tensor_tensor(sums[:, 1, v0:v1], centre_1[:, v0:v1], top[1][:, v0:v1], ADD)
+        weave(z_woven[:, 0:HALF_V, 0:2], sums[:, 0:2, 0:HALF_V], scalar_relu)
+        for (v0, v1), relu in zip(pieces[1:], (vector_relu, scalar_relu)):
+            weave(z_woven[:, v0:v1, :], sums[:, :, v0:v1], relu)
         result = [keep.tile([P, HALF_V], F32, name="result_%d" % h) for h in range(2)]
         for (v0, v1), copy in zip(pieces, (nc.scalar.copy, nc.scalar.copy, nc.vector.tensor_copy)):
             z_codes = keep.tile([P, v1 - v0], U32, name="z_codes_%d" % v0, align_bytes=64)

@@ -82,12 +82,11 @@ def tile_picked_edgecv_relu_e_kernel(
             nc.sync.dma_start(raw[:], x_rows[:, j, :])
             return raw
 
-        x_raw = [load_plane(0)]
-        offs_sb = load_list(offs, "offs_sb")
-        x_raw.extend(load_plane(j) for j in range(1, PACK))
         w2_raw = [keep.tile([P, PACK, HALF_H], F32, name="w2_raw_%d" % g, align_bytes=256) for g in range(2)]
-        for g in range(2):
-            nc.sync.dma_start(w2_raw[g][:], w2_rows[:, :, g * HALF_H : (g + 1) * HALF_H])
+        nc.sync.dma_start(w2_raw[0][:], w2_rows[:, :, 0:HALF_H])
+        offs_sb = load_list(offs, "offs_sb")
+        x_raw = [load_plane(j) for j in range(PACK)]
+        nc.sync.dma_start(w2_raw[1][:], w2_rows[:, :, HALF_H:H])
         pos_last = load_list(pos4, "pos_sb_3")
         pos_sb = [load_list(pos, "pos_sb_%d" % d) for d, pos in enumerate((pos1, pos2, pos3))] + [pos_last]
         w1_raw = held.tile([P, PACK, H], F32, name="w1_raw", offset=0, align_bytes=256)
@@ -106,10 +105,6 @@ def tile_picked_edgecv_relu_e_kernel(
         nc.vector.memset(warm_in[:], 0.0)
         nc.scalar.activation(warm_out[:], warm_in[:], RELU)
 
-        x_woven = keep.tile([P, S, PACK], BF16, align_bytes=64)
-        for j in range(PACK):
-            nc.vector.tensor_copy(x_woven[:, 0:VECTOR_POINTS, j], x_raw[j][:].indirect(entries(offs_sb, 0, VECTOR_POINTS)))
-            scalar_gather(x_woven[:, VECTOR_POINTS:S, j], x_raw[j][:].indirect(entries(offs_sb, VECTOR_POINTS, S)))
         DEALT = 8 * KIB
         NEAR = 16 * KIB
         x_codes = keep.tile([P, S], U32, align_bytes=64)
@@ -146,16 +141,22 @@ def tile_picked_edgecv_relu_e_kernel(
             for u in range(2):
                 quantize(high_codes, high_plane, u * P + g * HALF_P, flat(high[g][:, u : u + 1]))
 
-        quantize(x_codes, x_plane, 0, x_woven[:].rearrange("p c t -> p (c t)"))
         deal(w2_raw[0][:], low[0][:], 0, nc.vector.tensor_copy)
-        deal(w2_raw[0][:], high[0][:], 2, nc.scalar.copy)
+        deal(w2_raw[0][:], high[0][:], 2, nc.vector.tensor_copy)
         quantize(low_codes, low_plane, 0, flat(low[0][:]))
         quantize_high(0)
+        x_woven = keep.tile([P, S, PACK], BF16, align_bytes=64)
+        for j in range(PACK):
+            for c0, c1 in ((0, P), (P, VECTOR_POINTS)) if j == PACK - 1 else ((0, VECTOR_POINTS),):
+                nc.vector.tensor_copy(x_woven[:, c0:c1, j], x_raw[j][:].indirect(entries(offs_sb, c0, c1)))
+            scalar_gather(x_woven[:, VECTOR_POINTS:S, j], x_raw[j][:].indirect(entries(offs_sb, VECTOR_POINTS, S)))
+        for c0, c1 in ((0, P), (P, HALF_S), (HALF_S, S)):
+            quantize(x_codes, x_plane, c0, x_woven[:, c0:c1, :].rearrange("p c t -> p (c t)"))
+        for c0 in (0, HALF_S):
+            product(e_rows[0], low_codes, low_plane, 0, c0, c0 + HALF_S, nc.scalar.copy)
         deal(w2_raw[1][:], low[1][:], 0, nc.vector.tensor_copy)
         deal(w2_raw[1][:], high[1][:], 2, nc.vector.tensor_copy)
         quantize(low_codes, low_plane, P, flat(low[1][:]))
-        product(e_rows[0], low_codes, low_plane, 0, 0, HALF_S, nc.scalar.copy)
-        product(e_rows[0], low_codes, low_plane, 0, HALF_S, S, nc.scalar.copy)
         quantize_high(1)
         w1_dealt = held.tile([P, PACK, P, PACK], BF16, name="w1_dealt", offset=DEALT, align_bytes=64)
         gpsimd_copy(w1_dealt[:].rearrange("p t m j -> p m t j"), w1_raw[:].rearrange("p j (m t) -> p m t j", t=PACK))

@@ -149,11 +149,11 @@ def tile_picked_edgecv_relu_e_kernel(
         for j in range(PACK):
             for c0, c1 in ((0, P), (P, VECTOR_POINTS)) if j == PACK - 1 else ((0, VECTOR_POINTS),):
                 nc.vector.tensor_copy(x_woven[:, c0:c1, j], x_raw[j][:].indirect(entries(offs_sb, c0, c1)))
-            scalar_gather(x_woven[:, VECTOR_POINTS:S, j], x_raw[j][:].indirect(entries(offs_sb, VECTOR_POINTS, S)))
-        for c0, c1 in ((0, P), (P, HALF_S), (HALF_S, S)):
-            quantize(x_codes, x_plane, c0, x_woven[:, c0:c1, :].rearrange("p c t -> p (c t)"))
-        for c0 in (0, HALF_S):
-            product(e_rows[0], low_codes, low_plane, 0, c0, c0 + HALF_S, nc.scalar.copy)
+            for c0, c1 in ((VECTOR_POINTS, S - P), (S - P, S)) if j == PACK - 1 else ((VECTOR_POINTS, S),):
+                scalar_gather(x_woven[:, c0:c1, j], x_raw[j][:].indirect(entries(offs_sb, c0, c1)))
+        for c0 in (0, 2 * P, P, 3 * P):
+            quantize(x_codes, x_plane, c0, x_woven[:, c0 : c0 + P, :].rearrange("p c t -> p (c t)"))
+            product(e_rows[0], low_codes, low_plane, 0, c0, c0 + P, nc.scalar.copy)
         deal(w2_raw[1][:], low[1][:], 0, nc.vector.tensor_copy)
         deal(w2_raw[1][:], high[1][:], 2, nc.vector.tensor_copy)
         quantize(low_codes, low_plane, P, flat(low[1][:]))

from contextlib import ExitStack

import concourse.mybir as mybir

K, T, S, V, H, N = 512, 1024, 512, 256, 512, 128
FLOPS = 2 * K * H * S * 2 + 2 * H * N * V

F32 = mybir.dt.float32
BF16 = mybir.dt.bfloat16
U32 = mybir.dt.uint32
I32 = mybir.dt.int32
U16 = mybir.dt.uint16
U8 = mybir.dt.uint8
FP8X4 = mybir.dt.float8_e4m3fn_x4
ADD = mybir.AluOpType.add
MULT = mybir.AluOpType.mult
MAX = mybir.AluOpType.max
RELU = mybir.ActivationFunctionType.Relu
COPY = mybir.ActivationFunctionType.Copy

P = 128
PACK = 4
HALF_P = P // 2
HALF_S = S // 2
HALF_V = V // 2
HALF_H = H // 2
VECTOR_POINTS = 256
KIB = 1024


def tile_picked_edgecv_relu_e_kernel(
    tc, xT, w1, w2, w3_words, w3_scales, offs, cen, pos1, pos2, pos3, pos4, out
):
    nc = tc.nc
    with ExitStack() as ctx:
        keep = ctx.enter_context(tc.tile_pool(name="keep", bufs=1))
        held = ctx.enter_context(tc.tile_pool(name="held", bufs=1))
        psum = ctx.enter_context(tc.psum_pool(name="psum", bufs=1))

        def load_list(source, name):
            tile = keep.tile(list(source.shape), U16, name=name)
            nc.sync.dma_start(tile[:], source)
            return tile

        def entries(list_tile, first, last):
            return list_tile[:, first // 16 : last // 16]

        def weave(target, source, copy):
            copy(target.rearrange("p (c i) t -> p c t i", i=4), source.rearrange("p t (c i) -> p c t i", i=4))

        def scalar_relu(target, source):
            nc.scalar.activation(target, source, RELU)

        def vector_relu(target, source):
            nc.vector.tensor_scalar_max(target, source, 0.0)

        def scalar_gather(target, source):
            nc.scalar.activation(target, source, COPY)

        def gpsimd_copy(target, source):
            nc.gpsimd.tensor_scalar(target, source, 1.0, 0.0, MULT, ADD)

        def deal(raw, dealt, t0, copy):
            copy(
                dealt.rearrange("p t m j -> p m j t"),
                raw.rearrange("p j (m t) -> p m j t", t=PACK)[:, :, :, t0 : t0 + dealt.shape[1]],
            )

        def quantize(codes, plane, c0, values):
            cols = slice(c0, c0 + values.shape[1] // PACK)
            nc.vector.quantize_mx(out=codes[:, cols].bitcast(FP8X4), scales=plane[:, cols], in_=values)

        def larger(target, a, b):
            nc.vector.tensor_tensor(target, a, b, MAX)

        x_rows = xT.rearrange("(p j) c -> p j c", j=PACK)
        w1_rows = w1.rearrange("(p j) c -> p j c", j=PACK)
        w2_rows = w2.rearrange("(p j) c -> p j c", j=PACK)

        def load_plane(j):
            raw = keep.tile([P, T], F32, name="x_raw_%d" % j, align_bytes=256)
            nc.sync.dma_start(raw[:], x_rows[:, j, :])
            return raw

        w2_raw = [keep.tile([P, PACK, HALF_H], F32, name="w2_raw_%d" % g, align_bytes=256) for g in range(2)]
        nc.sync.dma_start(w2_raw[0][:], w2_rows[:, :, 0:HALF_H])
        offs_sb = load_list(offs, "offs_sb")
        x_raw = [load_plane(j) for j in range(PACK)]
        nc.sync.dma_start(w2_raw[1][:], w2_rows[:, :, HALF_H:H])
        pos_last = load_list(pos4, "pos_sb_3")
        pos_sb = [load_list(pos, "pos_sb_%d" % d) for d, pos in enumerate((pos1, pos2, pos3))] + [pos_last]
        w1_raw = held.tile([P, PACK, H], F32, name="w1_raw", offset=0, align_bytes=256)
        nc.sync.dma_start(w1_raw[:], w1_rows)
        cen_sb = load_list(cen, "cen_sb")

        w3_codes = keep.tile([P, N], U32, align_bytes=64)
        nc.sync.dma_start(w3_codes[:].bitcast(I32), w3_words[0].rearrange("p n t -> p (n t)").bitcast(I32))
        w3_plane = keep.tile([P, N], U8, align_bytes=64)
        nc.vector.memset(w3_plane[:].bitcast(I32), 0)
        for q in range(4):
            nc.sync.dma_start(w3_plane[32 * q : 32 * q + 4, :].bitcast(I32), w3_scales[0, 4 * q : 4 * q + 4, :].bitcast(I32))

        warm_in = keep.tile([P, 1], F32)
        warm_out = keep.tile([P, 1], F32)
        nc.vector.memset(warm_in[:], 0.0)
        nc.scalar.activation(warm_out[:], warm_in[:], RELU)

        DEALT = 8 * KIB
        NEAR = 16 * KIB
        x_codes = keep.tile([P, S], U32, align_bytes=64)
        x_plane = keep.tile([P, S], U8, align_bytes=64)

        w1_codes = keep.tile([P, H], U32, align_bytes=64)
        w1_plane = keep.tile([P, H], U8, align_bytes=64)
        low_codes = keep.tile([P, HALF_H], U32, align_bytes=64)
        low_plane = keep.tile([P, HALF_H], U8, align_bytes=64)
        high_codes = held.tile([P, HALF_H], U32, name="high_codes", offset=NEAR + 6 * KIB, align_bytes=64)
        high_plane = keep.tile([P, HALF_H], U8, align_bytes=64)
        e_rows = [keep.tile([P, S], F32, name="e_rows_%d" % t) for t in range(PACK)]

        def product(row, codes, plane, t, c0, c1, copy):
            acc = psum.tile([P, c1 - c0], F32, name="acc", tag="acc", bufs=8)
            nc.tensor.matmul_mx(
                out=acc[:],
                lhsT=codes[:, t * P : (t + 1) * P].bitcast(FP8X4),
                lhsT_scale=plane[:, t * P : (t + 1) * P],
                rhs=x_codes[:, c0:c1].bitcast(FP8X4),
                rhs_scale=x_plane[:, c0:c1],
                start=True,
                stop=True,
            )
            copy(row[:, c0:c1], acc[:])

        def flat(dealt):
            return dealt.rearrange("p t m j -> p (t m j)")

        low = [keep.tile([P, 2, HALF_P, PACK], BF16, name="low_%d" % g, align_bytes=64) for g in range(2)]
        high = [held.tile([P, 2, HALF_P, PACK], BF16, name="high_%d" % g, offset=DEALT + g * KIB, align_bytes=64) for g in range(2)]

        def quantize_high(g):
            for u in range(2):
                quantize(high_codes, high_plane, u * P + g * HALF_P, flat(high[g][:, u : u + 1]))

        deal(w2_raw[0][:], low[0][:], 0, nc.vector.tensor_copy)
        deal(w2_raw[0][:], high[0][:], 2, nc.vector.tensor_copy)
        quantize(low_codes, low_plane, 0, flat(low[0][:]))
        quantize_high(0)
        x_woven = keep.tile([P, S, PACK], BF16, align_bytes=64)
        for j in range(PACK):
            for c0, c1 in ((0, P), (P, VECTOR_POINTS)) if j == PACK - 1 else ((0, VECTOR_POINTS),):
                nc.vector.tensor_copy(x_woven[:, c0:c1, j], x_raw[j][:].indirect(entries(offs_sb, c0, c1)))
            for c0, c1 in ((VECTOR_POINTS, S - P), (S - P, S)) if j == PACK - 1 else ((VECTOR_POINTS, S),):
                scalar_gather(x_woven[:, c0:c1, j], x_raw[j][:].indirect(entries(offs_sb, c0, c1)))
        for c0 in (0, 2 * P, P, 3 * P):
            quantize(x_codes, x_plane, c0, x_woven[:, c0 : c0 + P, :].rearrange("p c t -> p (c t)"))
            product(e_rows[0], low_codes, low_plane, 0, c0, c0 + P, nc.scalar.copy)
        deal(w2_raw[1][:], low[1][:], 0, nc.vector.tensor_copy)
        deal(w2_raw[1][:], high[1][:], 2, nc.vector.tensor_copy)
        quantize(low_codes, low_plane, P, flat(low[1][:]))
        quantize_high(1)
        w1_dealt = held.tile([P, PACK, P, PACK], BF16, name="w1_dealt", offset=DEALT, align_bytes=64)
        gpsimd_copy(w1_dealt[:].rearrange("p t m j -> p m t j"), w1_raw[:].rearrange("p j (m t) -> p m t j", t=PACK))

        def fetch(target, t, d, v0, v1, gather):
            gather(target[:, v0:v1], e_rows[t][:].indirect(entries(pos_sb[d], v0, v1)))

        near_01 = held.tile([P, 2, 2, V], F32, name="near_01", offset=NEAR, align_bytes=64)
        far_01 = [held.tile([P, 2, V], F32, name="far_01_%d" % t, offset=NEAR + (4 + 2 * t) * KIB, align_bytes=64) for t in range(2)]
        near_23 = [keep.tile([P, 2, 2, V], F32, name="near_23_%d" % u) for u in range(2)]
        fetch(far_01[0][:, 1, :], 0, 3, 0, V, scalar_gather)
        product(e_rows[1], low_codes, low_plane, 1, 0, S, nc.scalar.copy)
        for t in range(2):
            product(e_rows[2 + t], high_codes, high_plane, t, 0, S, nc.scalar.copy)
        for d in range(2):
            fetch(near_01[:, 0, d, :], 0, d, 0, V, nc.vector.tensor_copy)
        fetch(far_01[0][:, 0, :], 0, 2, 0, V, nc.vector.tensor_copy)
        for d in range(2):
            fetch(near_01[:, 1, d, :], 1, d, 0, V, nc.vector.tensor_copy)
        for d in range(2):
            fetch(far_01[1][:, d, :], 1, 2 + d, 0, V, scalar_gather)
        for t in (2, 3):
            for d in (0, 2, 1, 3) if t == 3 else range(4):
                fetch(near_23[d // 2][:, t % 2, d % 2, :], t, d, 0, V, nc.vector.tensor_copy if d == 0 else scalar_gather)

        quantize(w1_codes, w1_plane, 0, flat(w1_dealt[:]))
        pair_01 = [held.tile([P, 2, V], F32, name="pair_01_%d" % g, offset=g * DEALT, align_bytes=64) for g in range(2)]
        for g in range(2):
            larger(pair_01[g][:], near_01[:, g], far_01[g][:])
        top = [keep.tile([P, V], F32, name="top_%d" % t) for t in range(PACK)]
        for g in range(2):
            crossed = keep.tile([P, V], F32, name="crossed_%d" % g)
            larger(crossed[:], pair_01[g][:, 0, :], pair_01[g][:, 1, :])
            for t in range(2):
                nc.sync.dma_start(top[t][HALF_P * g : HALF_P * (g + 1), :], crossed[HALF_P * t : HALF_P * (t + 1), :])

        pair_23 = held.tile([P, 4, V], F32, name="pair_23", offset=NEAR, align_bytes=64)
        slots = [near[:].rearrange("p t d v -> p (t d) v") for near in near_23]
        for s0, s1 in ((0, 3), (3, 4)):
            larger(pair_23[:, s0:s1], slots[0][:, s0:s1], slots[1][:, s0:s1])
        y_rows = [keep.tile([P, S], F32, name="y_rows_%d" % t) for t in range(PACK)]
        product(y_rows[2], w1_codes, w1_plane, 2, 0, S, nc.scalar.copy)

        sums = keep.tile([P, PACK, V], F32)

        def add_centre(t, v0, v1):
            nc.vector.tensor_tensor(sums[:, t, v0:v1], y_rows[t][:].indirect(entries(cen_sb, v0, v1)), top[t][:, v0:v1], ADD)

        for u in range(2):
            larger(top[2 + u][:], pair_23[:, 2 * u, :], pair_23[:, 2 * u + 1, :])
        for t in (3, 1, 0):
            product(y_rows[t], w1_codes, w1_plane, t, 0, S, nc.scalar.copy)
        centre_1 = keep.tile([P, V], F32)
        scalar_gather(centre_1[:], y_rows[1][:].indirect(cen_sb[:]))
        for t in (2, 3, 0):
            add_centre(t, 0, V)
        pieces = ((0, 128), (128, 192), (192, 256))
        z_woven = keep.tile([P, V, PACK], BF16, align_bytes=64)
        weave(z_woven[:, 0:HALF_V, 2:4], sums[:, 2:4, 0:HALF_V], scalar_relu)
        for v0, v1 in pieces:
            nc.vector.tensor_tensor(sums[:, 1, v0:v1], centre_1[:, v0:v1], top[1][:, v0:v1], ADD)
        weave(z_woven[:, 0:HALF_V, 0:2], sums[:, 0:2, 0:HALF_V], scalar_relu)
        for (v0, v1), relu in zip(pieces[1:], (vector_relu, scalar_relu)):
            weave(z_woven[:, v0:v1, :], sums[:, :, v0:v1], relu)
        result = [keep.tile([P, HALF_V], F32, name="result_%d" % h) for h in range(2)]
        for (v0, v1), copy in zip(pieces, (nc.scalar.copy, nc.scalar.copy, nc.vector.tensor_copy)):
            z_codes = keep.tile([P, v1 - v0], U32, name="z_codes_%d" % v0, align_bytes=64)
            z_plane = keep.tile([P, v1 - v0], U8, name="z_plane_%d" % v0, align_bytes=64)
            quantize(z_codes, z_plane, 0, z_woven[:, v0:v1, :].rearrange("p v t -> p (v t)"))
            acc_out = psum.tile([P, v1 - v0], F32, name="acc_out", tag="acc", bufs=8)
            nc.tensor.matmul_mx(
                out=acc_out[:],
                lhsT=w3_codes[:].bitcast(FP8X4),
                lhsT_scale=w3_plane[:],
                rhs=z_codes[:].bitcast(FP8X4),
                rhs_scale=z_plane[:],
                start=True,
                stop=True,
            )
            h = v0 // HALF_V
            copy(result[h][:, v0 - h * HALF_V : v1 - h * HALF_V], acc_out[:])
            if v1 % HALF_V == 0:
                nc.sync.dma_start(out[:, v1 - HALF_V : v1], result[h][:])
